import numpy as np
import ml_dtypes


def mxq(x, axis, fmt="e4m3"):
    dtype, down = {"e4m3": (ml_dtypes.float8_e4m3fn, 7), "e5m2": (ml_dtypes.float8_e5m2, 14)}[fmt]
    v = np.moveaxis(np.asarray(x, np.float32).astype(ml_dtypes.bfloat16).astype(np.float64), axis, -1)
    blocks = v.reshape(v.shape[:-1] + (-1, 32))
    amax = np.abs(blocks).max(-1, keepdims=True)
    byte = np.maximum(np.where(amax > 0, np.frexp(amax)[1] - 1 + 127, 0) - down, 1)
    scale = np.exp2(byte - 127.0)
    codes = (blocks / scale).astype(np.float32).astype(dtype).astype(np.float64)
    return np.moveaxis((codes * scale).reshape(v.shape), -1, axis)


WIDE = False


def mx_kscale(k):
    if not WIDE:
        return np.ones(k)
    levels = np.array([10, -10, 5, -5, 0])
    if k % 512:
        return np.exp2(np.random.permutation(np.resize(levels, k // 32))).repeat(32)
    a = np.empty((k // 512, 16))
    for p in range(k // 512):
        a[p, :8] = np.random.permutation(np.resize(levels, 8))
        for g in range(8):
            far = levels[np.abs(levels - a[p, g]) >= 10]
            a[p, g + 8] = far[np.random.randint(len(far))]
    return np.exp2(a.ravel()).repeat(32)


def f64(x):
    return np.asarray(x).astype(np.float64)


def striped(idx):
    return np.tile(np.asarray(idx).reshape(-1, 16).T, (8, 1)).astype(np.uint16)


def unstriped(offs):
    return offs[:16].T.reshape(-1).astype(np.int64)


E2M1 = np.array([0.0, 0.5, 1.0, 1.5, 2.0, 3.0, 4.0, 6.0, -0.0, -0.5, -1.0, -1.5, -2.0, -3.0, -4.0, -6.0])


def pack_weight(w, fmt):
    k, n = w.shape
    w = f64(np.asarray(w, np.float32).astype(ml_dtypes.bfloat16)).reshape(k // 32, 32, n)
    amax = np.abs(w).max(1)
    if fmt == "e4m3":
        byte = np.frexp(amax)[1] - 1 + 127 - 7
    else:
        mant, ex = np.frexp(amax / 6.0)
        byte = np.where(mant > 0.5, ex, ex - 1) + 127
    byte = np.clip(np.where(amax > 0, byte, 1), 1, 254)
    scaled = (w * np.exp2(127.0 - byte)[:, None, :]).reshape(k, n).astype(np.float32)
    by_word = np.ascontiguousarray(scaled.reshape(k // 512, 128, 4, n).transpose(0, 1, 3, 2))
    if fmt == "e4m3":
        words = by_word.astype(ml_dtypes.float8_e4m3fn).view(np.uint8)
    else:
        c = by_word.astype(ml_dtypes.float4_e2m1fn).view(np.uint8) & 0xF
        words = (c[..., 0::2] | (c[..., 1::2] << 4)).reshape(k // 512, 128, 2 * n)
    return np.ascontiguousarray(words), np.ascontiguousarray(byte.astype(np.uint8).reshape(k // 512, 16, n))


def unpack_weight(words, scales, fmt):
    g, _, n = scales.shape
    words = np.ascontiguousarray(words).reshape(g, 128, n, -1)
    if fmt == "e4m3":
        vals = words.view(ml_dtypes.float8_e4m3fn).astype(np.float64)
    else:
        nib = np.empty((g, 128, n, 4), np.uint8)
        nib[..., 0::2] = words & 0xF
        nib[..., 1::2] = words >> 4
        vals = E2M1[nib]
    vals = vals * np.repeat(np.exp2(scales.astype(np.float64) - 127.0), 8, axis=1)[..., None]
    return vals.transpose(0, 1, 3, 2).reshape(g * 512, n)


def sigmoid(v):
    return 1.0 / (1.0 + np.exp(-v))


B, N, T, D, NQ = 1, 512, 2048, 1024, 256


def setup_inputs():
    n = np.random.standard_normal
    idx = np.sort(np.random.permutation(T)[:B * N].reshape(B, N), axis=1).reshape(-1)
    s = mx_kscale(D)[:, None]
    kp = pack_weight(n((D, T)) / s, "e2m1")
    return {
        "qT": (n((B, D, NQ)) * s * (1.00 / np.sqrt(D))).astype(np.float32),
        "k_words": np.ascontiguousarray(kp[0].reshape(1, 2, 128, T, 2).transpose(0, 2, 3, 1, 4)).reshape(1, 128, T, 4),
        "k_scales": kp[1],
        "ts": np.tile(np.random.uniform(0.5, 2.0, 2048), (128, 1)).astype(np.float32),
        "pr": np.tile(np.random.uniform(0.1, 1.0, 2048), (128, 1)).astype(np.float32),
        "offs": striped(idx),
    }


def reference(qT, k_words, k_scales, ts, pr, offs):
    idx = unstriped(offs)
    pick = lambda x, which: x[:, which].reshape(x.shape[0], B, -1).transpose(1, 0, 2)
    k = unpack_weight(k_words.reshape(1, 128, T, 2, 2).transpose(0, 3, 1, 2, 4).reshape(2, 128, 2 * T), k_scales, "e2m1")
    kg = pick(k, idx)
    qq = mxq(f64(qT), 1, "e4m3")
    a = qq.transpose(0, 2, 1) @ kg
    y = sigmoid(a * pick(f64(ts), idx)[:, :1, :]) * pick(f64(pr), idx)[:, :1, :]
    return y

@@ -1,0 +1,120 @@
+from contextlib import ExitStack
+
+import concourse.mybir as mybir
+from concourse.masks import make_identity
+
+N, T, D, NQ = 512, 2048, 1024, 256
+FLOPS = 2 * NQ * N * D
+
+F32 = mybir.dt.float32
+BF16 = mybir.dt.bfloat16
+I32 = mybir.dt.int32
+U32 = mybir.dt.uint32
+U16 = mybir.dt.uint16
+U8 = mybir.dt.uint8
+FP8X4 = mybir.dt.float8_e4m3fn_x4
+FP4X4 = mybir.dt.float4_e2m1fn_x4
+MULT = mybir.AluOpType.mult
+SIGMOID = mybir.ActivationFunctionType.Sigmoid
+
+P = 128
+PACK = 4
+PASSES = D // (P * PACK)
+HALVES = NQ // P
+BLOCKS = N // P
+ROW = P - 1
+SHIFT = 16
+
+
+def tile_attend_sigprior_srt_kernel(tc, qT, k_words, k_scales, ts, pr, offs, out):
+    nc = tc.nc
+    with ExitStack() as ctx:
+        keep = ctx.enter_context(tc.tile_pool(name="keep", bufs=1))
+        psum = ctx.enter_context(tc.psum_pool(name="psum", bufs=1))
+
+        offsets = keep.tile([P, N // 16], U16, name="offsets")
+        scale_pool = keep.tile([P, T // 4], I32, name="scale_pool", align_bytes=64)
+        ts_pool = keep.tile([P, T], F32, name="ts_pool", align_bytes=64)
+        pr_pool = keep.tile([P, T], F32, name="pr_pool", align_bytes=64)
+        word_pool = keep.tile([P, T], I32, name="word_pool", align_bytes=64)
+        plane1 = keep.tile([P, N // 4], I32, name="plane1", align_bytes=64)
+        ident = keep.tile([P, P], F32, name="ident", align_bytes=64)
+
+        nc.vector.memset(scale_pool[:], 0)
+        nc.vector.memset(ts_pool[0:ROW, :], 0.0)
+        nc.vector.memset(plane1[:], 0)
+        make_identity(nc, ident[:])
+
+        nc.sync.dma_start(offsets[:], offs)
+        nc.sync.dma_start(ts_pool[ROW:P, :], ts[0:1, :])
+        scale_rows = k_scales.bitcast(I32).rearrange("o (g r) t -> r g o t", r=4)
+        for r in range(4):
+            nc.sync.dma_start(scale_pool[r:P:SHIFT, :], scale_rows[r])
+        nc.sync.dma_start(word_pool[:], k_words[0].rearrange("p t b -> p (t b)").bitcast(I32))
+        q_raw = []
+        for o in range(PASSES):
+            raw = keep.tile([P, PACK, NQ], F32, name="q_raw%d" % o, align_bytes=64)
+            nc.sync.dma_start(raw[:], qT[0, o * P * PACK : (o + 1) * P * PACK, :].rearrange("(p j) w -> p j w", j=PACK))
+            q_raw.append(raw)
+
+        ts_picked = keep.tile([P, N], F32, name="ts_picked", align_bytes=64)
+        nc.vector.tensor_copy(ts_picked[:], ts_pool[:].indirect(offsets[:]))
+        plane0 = keep.tile([P, N], U8, name="plane0", align_bytes=64)
+        nc.vector.tensor_copy(plane0[:], scale_pool[:].bitcast(U8).indirect(offsets[:]))
+        nc.sync.dma_start(plane1[0 : P - SHIFT, :], plane0[SHIFT:P, :].bitcast(I32))
+        nc.sync.dma_start(pr_pool[:], pr)
+        planes = [plane0[:], plane1[:].bitcast(U8)]
+
+        ts_turned = psum.tile([P, BLOCKS, P], F32, name="ts_turned")
+        for j in range(BLOCKS):
+            nc.tensor.transpose(ts_turned[:, j, :], ts_picked[:, j * P : (j + 1) * P], ident[:])
+        ts_cols = keep.tile([P, BLOCKS], F32, name="ts_cols", align_bytes=64)
+        nc.scalar.copy(ts_cols[:], ts_turned[:, :, ROW])
+        ts_psum = psum.tile([P, N], F32, name="ts_psum")
+        for j in range(BLOCKS):
+            nc.tensor.transpose(ts_psum[:, j * P : (j + 1) * P], ts_cols[:, j : j + 1].to_broadcast([P, P]), ident[:])
+        ts_wide = keep.tile([P, N], F32, name="ts_wide", align_bytes=64)
+        nc.scalar.copy(ts_wide[:], ts_psum[:])
+
+        words = keep.tile([P, N], U32, name="words", align_bytes=64)
+        nc.vector.tensor_copy(words[:], word_pool[:].bitcast(U32).indirect(offsets[:]))
+        k_codes = keep.tile([P, PASSES, N], U16, name="k_codes", align_bytes=64)
+
+        acc = [psum.tile([P, N], F32, name="acc%d" % h) for h in range(HALVES)]
+        for o in range(PASSES):
+            grouped = []
+            for h in range(HALVES):
+                g = keep.tile([P, P, PACK], BF16, name="q_grouped%d%d" % (o, h), align_bytes=64)
+                src = q_raw[o][:, :, h * P : (h + 1) * P].rearrange("p j w -> p w j")
+                if h == 0:
+                    nc.vector.tensor_copy(g[:], src)
+                else:
+                    nc.scalar.copy(g[:], src)
+                grouped.append(g)
+            if o == 0:
+                nc.vector.tensor_copy(k_codes[:], words[:].bitcast(U16).rearrange("p (n o) -> p o n", o=PASSES))
+            for h in range(HALVES):
+                codes = keep.tile([P, P], U32, name="q_codes%d%d" % (o, h), align_bytes=64)
+                scales = keep.tile([P, P], U8, name="q_scales%d%d" % (o, h), align_bytes=64)
+                nc.vector.quantize_mx(out=codes[:].bitcast(FP8X4), scales=scales[:], in_=grouped[h][:].rearrange("p w j -> p (w j)"))
+                nc.tensor.matmul_mx(
+                    out=acc[h][:],
+                    lhsT=codes[:].bitcast(FP8X4),
+                    lhsT_scale=scales[:],
+                    rhs=k_codes[:, o, :].bitcast(FP4X4),
+                    rhs_scale=planes[o],
+                    start=(o == 0),
+                    stop=(o == PASSES - 1),
+                )
+
+        gates = []
+        for h in range(HALVES):
+            s = keep.tile([P, N], F32, name="scaled%d" % h, align_bytes=64)
+            nc.vector.tensor_tensor(s[:], acc[h][:], ts_wide[:], MULT)
+            g = keep.tile([P, N], F32, name="gate%d" % h, align_bytes=64)
+            nc.scalar.activation(g[:], s[:], SIGMOID)
+            gates.append(g)
+        for h, lo, hi in ((0, 0, N), (1, 0, N // 2), (1, N // 2, N)):
+            res = keep.tile([P, hi - lo], F32, name="result%d_%d" % (h, lo), align_bytes=64)
+            nc.vector.tensor_tensor(res[:], pr_pool[:].indirect(offsets[:, lo // 16 : hi // 16]), gates[h][:, lo:hi], MULT)
+            nc.sync.dma_start(out[0, h * P : (h + 1) * P, lo:hi], res[:])

@@ -33,9 +33,8 @@ def tile_attend_sigprior_srt_kernel(tc, qT, k_words, k_scales, ts, pr, offs, out
         psum = ctx.enter_context(tc.psum_pool(name="psum", bufs=1))
 
         offsets = keep.tile([P, N // 16], U16, name="offsets")
-        scale_pool = keep.tile([P, T // 4], I32, name="scale_pool", align_bytes=64)
+        scale_pool = keep.tile([P, T // 4], I32, name="scale_pool", tag="shared", align_bytes=64)
         ts_pool = keep.tile([P, T], F32, name="ts_pool", align_bytes=64)
-        pr_pool = keep.tile([P, T], F32, name="pr_pool", align_bytes=64)
         word_pool = keep.tile([P, T], I32, name="word_pool", align_bytes=64)
         plane1 = keep.tile([P, N // 4], I32, name="plane1", align_bytes=64)
         ident = keep.tile([P, P], F32, name="ident", align_bytes=64)
@@ -44,6 +43,8 @@ def tile_attend_sigprior_srt_kernel(tc, qT, k_words, k_scales, ts, pr, offs, out
         nc.vector.memset(ts_pool[0:ROW, :], 0.0)
         nc.vector.memset(plane1[:], 0)
         make_identity(nc, ident[:])
+        warm = keep.tile([P, 1], F32, name="warm")
+        nc.scalar.activation(warm[:], ident[:, 0:1], SIGMOID)
 
         nc.sync.dma_start(offsets[:], offs)
         nc.sync.dma_start(ts_pool[ROW:P, :], ts[0:1, :])
@@ -62,6 +63,7 @@ def tile_attend_sigprior_srt_kernel(tc, qT, k_words, k_scales, ts, pr, offs, out
         plane0 = keep.tile([P, N], U8, name="plane0", align_bytes=64)
         nc.vector.tensor_copy(plane0[:], scale_pool[:].bitcast(U8).indirect(offsets[:]))
         nc.sync.dma_start(plane1[0 : P - SHIFT, :], plane0[SHIFT:P, :].bitcast(I32))
+        pr_pool = keep.tile([P, T], F32, name="pr_pool", tag="shared", align_bytes=64)
         nc.sync.dma_start(pr_pool[:], pr)
         planes = [plane0[:], plane1[:].bitcast(U8)]
 
@@ -86,7 +88,7 @@ def tile_attend_sigprior_srt_kernel(tc, qT, k_words, k_scales, ts, pr, offs, out
             for h in range(HALVES):
                 g = keep.tile([P, P, PACK], BF16, name="q_grouped%d%d" % (o, h), align_bytes=64)
                 src = q_raw[o][:, :, h * P : (h + 1) * P].rearrange("p j w -> p w j")
-                if h == 0:
+                if h == 0 or o == 1:
                     nc.vector.tensor_copy(g[:], src)
                 else:
                     nc.scalar.copy(g[:], src)

@@ -40,21 +40,26 @@ def tile_attend_sigprior_srt_kernel(tc, qT, k_words, k_scales, ts, pr, offs, out
         ident = keep.tile([P, P], F32, name="ident", align_bytes=64)
 
         nc.vector.memset(scale_pool[:], 0)
-        nc.vector.memset(ts_pool[0:ROW, :], 0.0)
         nc.vector.memset(plane1[:], 0)
+        nc.gpsimd.memset(ts_pool[0:ROW, 0 : T // 2], 0.0)
+        nc.vector.memset(ts_pool[0:ROW, T // 2 : T], 0.0)
         make_identity(nc, ident[:])
         warm = keep.tile([P, 1], F32, name="warm")
         nc.scalar.activation(warm[:], ident[:, 0:1], SIGMOID)
 
+        idle = psum.tile([P, BLOCKS, P], F32, name="idle")
+
         nc.sync.dma_start(offsets[:], offs)
         nc.sync.dma_start(ts_pool[ROW:P, :], ts[0:1, :])
+        word_rows = k_words[0].rearrange("p t b -> p (t b)").bitcast(I32)
+        nc.sync.dma_start(word_pool[:, 0:512], word_rows[:, 0:512])
         scale_rows = k_scales.bitcast(I32).rearrange("o (g r) t -> r g o t", r=4)
         for r in range(4):
             nc.sync.dma_start(scale_pool[r:P:SHIFT, :], scale_rows[r])
-        nc.sync.dma_start(word_pool[:], k_words[0].rearrange("p t b -> p (t b)").bitcast(I32))
+        nc.sync.dma_start(word_pool[:, 512:T], word_rows[:, 512:T])
         q_raw = []
         for o in range(PASSES):
-            raw = keep.tile([P, PACK, NQ], F32, name="q_raw%d" % o, align_bytes=64)
+            raw = keep.tile([P, PACK, NQ], F32, name="q_raw%d" % o, tag="q_raw%d" % o, align_bytes=64)
             nc.sync.dma_start(raw[:], qT[0, o * P * PACK : (o + 1) * P * PACK, :].rearrange("(p j) w -> p j w", j=PACK))
             q_raw.append(raw)
 
@@ -71,43 +76,58 @@ def tile_attend_sigprior_srt_kernel(tc, qT, k_words, k_scales, ts, pr, offs, out
         for j in range(BLOCKS):
             nc.tensor.transpose(ts_turned[:, j, :], ts_picked[:, j * P : (j + 1) * P], ident[:])
         ts_cols = keep.tile([P, BLOCKS], F32, name="ts_cols", align_bytes=64)
-        nc.scalar.copy(ts_cols[:], ts_turned[:, :, ROW])
+        nc.vector.tensor_copy(ts_cols[:], ts_turned[:, :, ROW])
         ts_psum = psum.tile([P, N], F32, name="ts_psum")
         for j in range(BLOCKS):
             nc.tensor.transpose(ts_psum[:, j * P : (j + 1) * P], ts_cols[:, j : j + 1].to_broadcast([P, P]), ident[:])
-        ts_wide = keep.tile([P, N], F32, name="ts_wide", align_bytes=64)
-        nc.scalar.copy(ts_wide[:], ts_psum[:])
+        for i in range(12):
+            nc.tensor.transpose(idle[:, i % BLOCKS, :], ts_picked[:, 0:P], ident[:])
 
-        words = keep.tile([P, N], U32, name="words", align_bytes=64)
-        nc.vector.tensor_copy(words[:], word_pool[:].bitcast(U32).indirect(offsets[:]))
         k_codes = keep.tile([P, PASSES, N], U16, name="k_codes", align_bytes=64)
+        part = N // 2
+        words = []
+        for a in range(2):
+            w = keep.tile([P, part], U32, name="words%d" % a, tag="words%d" % a, align_bytes=64)
+            nc.vector.tensor_copy(w[:], word_pool[:].bitcast(U32).indirect(offsets[:, a * part // 16 : (a + 1) * part // 16]))
+            words.append(w)
+        for a in range(2):
+            nc.vector.tensor_copy(
+                k_codes[:, :, a * part : (a + 1) * part], words[a][:].bitcast(U16).rearrange("p (n o) -> p o n", o=PASSES)
+            )
 
         acc = [psum.tile([P, N], F32, name="acc%d" % h) for h in range(HALVES)]
-        for o in range(PASSES):
-            grouped = []
-            for h in range(HALVES):
-                g = keep.tile([P, P, PACK], BF16, name="q_grouped%d%d" % (o, h), align_bytes=64)
-                src = q_raw[o][:, :, h * P : (h + 1) * P].rearrange("p j w -> p w j")
-                if h == 0 or o == 1:
-                    nc.vector.tensor_copy(g[:], src)
-                else:
-                    nc.scalar.copy(g[:], src)
-                grouped.append(g)
-            if o == 0:
-                nc.vector.tensor_copy(k_codes[:], words[:].bitcast(U16).rearrange("p (n o) -> p o n", o=PASSES))
-            for h in range(HALVES):
-                codes = keep.tile([P, P], U32, name="q_codes%d%d" % (o, h), align_bytes=64)
-                scales = keep.tile([P, P], U8, name="q_scales%d%d" % (o, h), align_bytes=64)
-                nc.vector.quantize_mx(out=codes[:].bitcast(FP8X4), scales=scales[:], in_=grouped[h][:].rearrange("p w j -> p (w j)"))
-                nc.tensor.matmul_mx(
-                    out=acc[h][:],
-                    lhsT=codes[:].bitcast(FP8X4),
-                    lhsT_scale=scales[:],
-                    rhs=k_codes[:, o, :].bitcast(FP4X4),
-                    rhs_scale=planes[o],
-                    start=(o == 0),
-                    stop=(o == PASSES - 1),
-                )
+        grouped = [
+            keep.tile([P, HALVES, P, PACK], BF16, name="grouped%d" % o, tag=tag, align_bytes=64)
+            for o, tag in enumerate(("grouped0", "words1"))
+        ]
+
+        def interleave(o, h, copy):
+            copy(grouped[o][:, h], q_raw[o][:, :, h * P : (h + 1) * P].rearrange("p j w -> p w j"))
+
+        def score(o, h, tag):
+            codes = keep.tile([P, P], U32, name="q_codes%d%d" % (o, h), tag=tag, align_bytes=64)
+            scales = keep.tile([P, P], U8, name="q_scales%d%d" % (o, h), align_bytes=64)
+            nc.vector.quantize_mx(out=codes[:].bitcast(FP8X4), scales=scales[:], in_=grouped[o][:, h].rearrange("p w j -> p (w j)"))
+            nc.tensor.matmul_mx(
+                out=acc[h][:],
+                lhsT=codes[:].bitcast(FP8X4),
+                lhsT_scale=scales[:],
+                rhs=k_codes[:, o, :].bitcast(FP4X4),
+                rhs_scale=planes[o],
+                start=(o == 0),
+                stop=(o == PASSES - 1),
+            )
+
+        for h in range(HALVES):
+            interleave(0, h, nc.scalar.copy)
+        ts_wide = keep.tile([P, N], F32, name="ts_wide", align_bytes=64)
+        nc.scalar.copy(ts_wide[:], ts_psum[:])
+        score(0, 0, "words0")
+        for h in range(HALVES):
+            interleave(1, h, nc.vector.tensor_copy)
+        score(1, 0, "codes10")
+        score(0, 1, "q_raw1")
+        score(1, 1, "codes11")
 
         gates = []
         for h in range(HALVES):

@@ -24,6 +24,8 @@ HALVES = NQ // P
 BLOCKS = N // P
 ROW = P - 1
 SHIFT = 16
+PARTS = 2
+PART = N // PARTS
 
 
 def tile_attend_sigprior_srt_kernel(tc, qT, k_words, k_scales, ts, pr, offs, out):
@@ -33,81 +35,86 @@ def tile_attend_sigprior_srt_kernel(tc, qT, k_words, k_scales, ts, pr, offs, out
         psum = ctx.enter_context(tc.psum_pool(name="psum", bufs=1))
 
         offsets = keep.tile([P, N // 16], U16, name="offsets")
-        scale_pool = keep.tile([P, T // 4], I32, name="scale_pool", tag="shared", align_bytes=64)
+        scale_pool = keep.tile([P, T // 4], I32, name="scale_pool", align_bytes=64)
         ts_pool = keep.tile([P, T], F32, name="ts_pool", align_bytes=64)
+        pr_pool = keep.tile([P, T], F32, name="pr_pool", align_bytes=64)
         word_pool = keep.tile([P, T], I32, name="word_pool", align_bytes=64)
         plane1 = keep.tile([P, N // 4], I32, name="plane1", align_bytes=64)
         ident = keep.tile([P, P], F32, name="ident", align_bytes=64)
 
         nc.vector.memset(scale_pool[:], 0)
+        nc.vector.memset(ts_pool[0:ROW, :], 0.0)
+        nc.vector.memset(pr_pool[0:ROW, :], 0.0)
         nc.vector.memset(plane1[:], 0)
-        nc.gpsimd.memset(ts_pool[0:ROW, 0 : T // 2], 0.0)
-        nc.vector.memset(ts_pool[0:ROW, T // 2 : T], 0.0)
         make_identity(nc, ident[:])
         warm = keep.tile([P, 1], F32, name="warm")
         nc.scalar.activation(warm[:], ident[:, 0:1], SIGMOID)
 
-        idle = psum.tile([P, BLOCKS, P], F32, name="idle")
-
         nc.sync.dma_start(offsets[:], offs)
         nc.sync.dma_start(ts_pool[ROW:P, :], ts[0:1, :])
-        word_rows = k_words[0].rearrange("p t b -> p (t b)").bitcast(I32)
-        nc.sync.dma_start(word_pool[:, 0:512], word_rows[:, 0:512])
+        nc.sync.dma_start(pr_pool[ROW:P, :], pr[0:1, :])
         scale_rows = k_scales.bitcast(I32).rearrange("o (g r) t -> r g o t", r=4)
         for r in range(4):
             nc.sync.dma_start(scale_pool[r:P:SHIFT, :], scale_rows[r])
-        nc.sync.dma_start(word_pool[:, 512:T], word_rows[:, 512:T])
+        nc.sync.dma_start(word_pool[:], k_words[0].rearrange("p t b -> p (t b)").bitcast(I32))
         q_raw = []
         for o in range(PASSES):
-            raw = keep.tile([P, PACK, NQ], F32, name="q_raw%d" % o, tag="q_raw%d" % o, align_bytes=64)
+            raw = keep.tile([P, PACK, NQ], F32, name="q_raw%d" % o, align_bytes=64)
             nc.sync.dma_start(raw[:], qT[0, o * P * PACK : (o + 1) * P * PACK, :].rearrange("(p j) w -> p j w", j=PACK))
             q_raw.append(raw)
 
-        ts_picked = keep.tile([P, N], F32, name="ts_picked", align_bytes=64)
-        nc.vector.tensor_copy(ts_picked[:], ts_pool[:].indirect(offsets[:]))
+        def pick_and_turn(name, pool):
+            picked = keep.tile([P, N], F32, name=name + "_picked", align_bytes=64)
+            nc.vector.tensor_copy(picked[:], pool[:].indirect(offsets[:]))
+            turned = psum.tile([P, BLOCKS, P], F32, name=name + "_turned")
+            for j in range(BLOCKS):
+                nc.tensor.transpose(turned[:, j, :], picked[:, j * P : (j + 1) * P], ident[:])
+            return turned
+
+        def spread(name, turned):
+            cols = keep.tile([P, BLOCKS], F32, name=name + "_cols", align_bytes=64)
+            nc.vector.tensor_copy(cols[:], turned[:, :, ROW])
+            wide = psum.tile([P, N], F32, name=name + "_wide")
+            for j in range(BLOCKS):
+                nc.tensor.transpose(wide[:, j * P : (j + 1) * P], cols[:, j : j + 1].to_broadcast([P, P]), ident[:])
+            return wide
+
+        ts_turned = pick_and_turn("ts", ts_pool)
+        pr_turned = pick_and_turn("pr", pr_pool)
         plane0 = keep.tile([P, N], U8, name="plane0", align_bytes=64)
         nc.vector.tensor_copy(plane0[:], scale_pool[:].bitcast(U8).indirect(offsets[:]))
         nc.sync.dma_start(plane1[0 : P - SHIFT, :], plane0[SHIFT:P, :].bitcast(I32))
-        pr_pool = keep.tile([P, T], F32, name="pr_pool", tag="shared", align_bytes=64)
-        nc.sync.dma_start(pr_pool[:], pr)
         planes = [plane0[:], plane1[:].bitcast(U8)]
-
-        ts_turned = psum.tile([P, BLOCKS, P], F32, name="ts_turned")
-        for j in range(BLOCKS):
-            nc.tensor.transpose(ts_turned[:, j, :], ts_picked[:, j * P : (j + 1) * P], ident[:])
-        ts_cols = keep.tile([P, BLOCKS], F32, name="ts_cols", align_bytes=64)
-        nc.vector.tensor_copy(ts_cols[:], ts_turned[:, :, ROW])
-        ts_psum = psum.tile([P, N], F32, name="ts_psum")
-        for j in range(BLOCKS):
-            nc.tensor.transpose(ts_psum[:, j * P : (j + 1) * P], ts_cols[:, j : j + 1].to_broadcast([P, P]), ident[:])
-        for i in range(12):
-            nc.tensor.transpose(idle[:, i % BLOCKS, :], ts_picked[:, 0:P], ident[:])
+        ts_psum = spread("ts", ts_turned)
 
         k_codes = keep.tile([P, PASSES, N], U16, name="k_codes", align_bytes=64)
-        part = N // 2
         words = []
-        for a in range(2):
-            w = keep.tile([P, part], U32, name="words%d" % a, tag="words%d" % a, align_bytes=64)
-            nc.vector.tensor_copy(w[:], word_pool[:].bitcast(U32).indirect(offsets[:, a * part // 16 : (a + 1) * part // 16]))
+
+        def gather_words(a):
+            w = keep.tile([P, PART], U32, name="words%d" % a, tag="words%d" % a, align_bytes=64)
+            nc.vector.tensor_copy(w[:], word_pool[:].bitcast(U32).indirect(offsets[:, a * PART // 16 : (a + 1) * PART // 16]))
             words.append(w)
-        for a in range(2):
+
+        gather_words(0)
+        pr_wide = spread("pr", pr_turned)
+        gather_words(1)
+        for a in range(PARTS):
             nc.vector.tensor_copy(
-                k_codes[:, :, a * part : (a + 1) * part], words[a][:].bitcast(U16).rearrange("p (n o) -> p o n", o=PASSES)
+                k_codes[:, :, a * PART : (a + 1) * PART], words[a][:].bitcast(U16).rearrange("p (n o) -> p o n", o=PASSES)
             )
 
         acc = [psum.tile([P, N], F32, name="acc%d" % h) for h in range(HALVES)]
-        grouped = [
-            keep.tile([P, HALVES, P, PACK], BF16, name="grouped%d" % o, tag=tag, align_bytes=64)
-            for o, tag in enumerate(("grouped0", "words1"))
-        ]
+        grouped = {}
 
-        def interleave(o, h, copy):
-            copy(grouped[o][:, h], q_raw[o][:, :, h * P : (h + 1) * P].rearrange("p j w -> p w j"))
+        def interleave(o, h, copy, tag):
+            g = keep.tile([P, P, PACK], BF16, name="grouped%d%d" % (o, h), tag=tag, align_bytes=64)
+            copy(g[:], q_raw[o][:, :, h * P : (h + 1) * P].rearrange("p j w -> p w j"))
+            grouped[o, h] = g
 
         def score(o, h, tag):
             codes = keep.tile([P, P], U32, name="q_codes%d%d" % (o, h), tag=tag, align_bytes=64)
             scales = keep.tile([P, P], U8, name="q_scales%d%d" % (o, h), align_bytes=64)
-            nc.vector.quantize_mx(out=codes[:].bitcast(FP8X4), scales=scales[:], in_=grouped[o][:, h].rearrange("p w j -> p (w j)"))
+            nc.vector.quantize_mx(out=codes[:].bitcast(FP8X4), scales=scales[:], in_=grouped[o, h][:].rearrange("p w j -> p (w j)"))
             nc.tensor.matmul_mx(
                 out=acc[h][:],
                 lhsT=codes[:].bitcast(FP8X4),
@@ -118,25 +125,26 @@ def tile_attend_sigprior_srt_kernel(tc, qT, k_words, k_scales, ts, pr, offs, out
                 stop=(o == PASSES - 1),
             )
 
-        for h in range(HALVES):
-            interleave(0, h, nc.scalar.copy)
-        ts_wide = keep.tile([P, N], F32, name="ts_wide", align_bytes=64)
+        interleave(0, 0, nc.scalar.copy, "grouped00")
+        interleave(0, 1, nc.scalar.copy, "grouped01")
+        interleave(1, 1, nc.scalar.copy, "grouped11")
+        ts_wide = keep.tile([P, N], F32, name="ts_wide_sb", align_bytes=64)
         nc.scalar.copy(ts_wide[:], ts_psum[:])
         score(0, 0, "words0")
-        for h in range(HALVES):
-            interleave(1, h, nc.vector.tensor_copy)
+        interleave(1, 0, nc.vector.tensor_copy, "words1")
+        score(0, 1, "grouped00")
         score(1, 0, "codes10")
-        score(0, 1, "q_raw1")
-        score(1, 1, "codes11")
+        score(1, 1, "words1")
 
+        pieces = [(h, slice(a * PART, (a + 1) * PART)) for h in range(HALVES) for a in range(PARTS)]
         gates = []
-        for h in range(HALVES):
-            s = keep.tile([P, N], F32, name="scaled%d" % h, align_bytes=64)
-            nc.vector.tensor_tensor(s[:], acc[h][:], ts_wide[:], MULT)
-            g = keep.tile([P, N], F32, name="gate%d" % h, align_bytes=64)
+        for i, (h, cols) in enumerate(pieces):
+            s = keep.tile([P, PART], F32, name="scaled%d" % i, align_bytes=64)
+            nc.vector.tensor_tensor(s[:], acc[h][:, cols], ts_wide[:, cols], MULT)
+            g = keep.tile([P, PART], F32, name="gate%d" % i, align_bytes=64)
             nc.scalar.activation(g[:], s[:], SIGMOID)
             gates.append(g)
-        for h, lo, hi in ((0, 0, N), (1, 0, N // 2), (1, N // 2, N)):
-            res = keep.tile([P, hi - lo], F32, name="result%d_%d" % (h, lo), align_bytes=64)
-            nc.vector.tensor_tensor(res[:], pr_pool[:].indirect(offsets[:, lo // 16 : hi // 16]), gates[h][:, lo:hi], MULT)
-            nc.sync.dma_start(out[0, h * P : (h + 1) * P, lo:hi], res[:])
+        for i, (h, cols) in enumerate(pieces):
+            res = keep.tile([P, PART], F32, name="result%d" % i, align_bytes=64)
+            nc.vector.tensor_tensor(res[:], gates[i][:], pr_wide[:, cols], MULT)
+            nc.sync.dma_start(out[0, h * P : (h + 1) * P, cols], res[:])

@@ -22,6 +22,8 @@ PACK = 4
 PASSES = D // (P * PACK)
 HALVES = NQ // P
 BLOCKS = N // P
+GROUP = 16
+SCALE_ROWS = 4
 ROW = P - 1
 SHIFT = 16
 PARTS = 2
@@ -34,7 +36,7 @@ def tile_attend_sigprior_srt_kernel(tc, qT, k_words, k_scales, ts, pr, offs, out
         keep = ctx.enter_context(tc.tile_pool(name="keep", bufs=1))
         psum = ctx.enter_context(tc.psum_pool(name="psum", bufs=1))
 
-        offsets = keep.tile([P, N // 16], U16, name="offsets")
+        offsets = keep.tile([P, N // GROUP], U16, name="offsets")
         scale_pool = keep.tile([P, T // 4], I32, name="scale_pool", align_bytes=64)
         ts_pool = keep.tile([P, T], F32, name="ts_pool", align_bytes=64)
         pr_pool = keep.tile([P, T], F32, name="pr_pool", align_bytes=64)
@@ -47,20 +49,19 @@ def tile_attend_sigprior_srt_kernel(tc, qT, k_words, k_scales, ts, pr, offs, out
         nc.vector.memset(pr_pool[0:ROW, :], 0.0)
         nc.vector.memset(plane1[:], 0)
         make_identity(nc, ident[:])
-        warm = keep.tile([P, 1], F32, name="warm")
-        nc.scalar.activation(warm[:], ident[:, 0:1], SIGMOID)
 
         nc.sync.dma_start(offsets[:], offs)
         nc.sync.dma_start(ts_pool[ROW:P, :], ts[0:1, :])
         nc.sync.dma_start(pr_pool[ROW:P, :], pr[0:1, :])
-        scale_rows = k_scales.bitcast(I32).rearrange("o (g r) t -> r g o t", r=4)
-        for r in range(4):
+        scale_rows = k_scales.bitcast(I32).rearrange("o (g r) t -> r g o t", r=SCALE_ROWS)
+        for r in range(SCALE_ROWS):
             nc.sync.dma_start(scale_pool[r:P:SHIFT, :], scale_rows[r])
         nc.sync.dma_start(word_pool[:], k_words[0].rearrange("p t b -> p (t b)").bitcast(I32))
         q_raw = []
         for o in range(PASSES):
-            raw = keep.tile([P, PACK, NQ], F32, name="q_raw%d" % o, align_bytes=64)
-            nc.sync.dma_start(raw[:], qT[0, o * P * PACK : (o + 1) * P * PACK, :].rearrange("(p j) w -> p j w", j=PACK))
+            raw = keep.tile([P, PACK, NQ], F32, name="q_raw%d" % o, tag="q_raw%d" % o, align_bytes=64)
+            rows = qT[0, o * P * PACK : (o + 1) * P * PACK, :]
+            nc.sync.dma_start(raw[:], rows.rearrange("(p t) q -> p t q", t=PACK))
             q_raw.append(raw)
 
         def pick_and_turn(name, pool):
@@ -73,7 +74,7 @@ def tile_attend_sigprior_srt_kernel(tc, qT, k_words, k_scales, ts, pr, offs, out
 
         def spread(name, turned):
             cols = keep.tile([P, BLOCKS], F32, name=name + "_cols", align_bytes=64)
-            nc.vector.tensor_copy(cols[:], turned[:, :, ROW])
+            nc.scalar.copy(cols[:], turned[:, :, ROW])
             wide = psum.tile([P, N], F32, name=name + "_wide")
             for j in range(BLOCKS):
                 nc.tensor.transpose(wide[:, j * P : (j + 1) * P], cols[:, j : j + 1].to_broadcast([P, P]), ident[:])
@@ -81,42 +82,42 @@ def tile_attend_sigprior_srt_kernel(tc, qT, k_words, k_scales, ts, pr, offs, out
 
         ts_turned = pick_and_turn("ts", ts_pool)
         pr_turned = pick_and_turn("pr", pr_pool)
+
         plane0 = keep.tile([P, N], U8, name="plane0", align_bytes=64)
         nc.vector.tensor_copy(plane0[:], scale_pool[:].bitcast(U8).indirect(offsets[:]))
         nc.sync.dma_start(plane1[0 : P - SHIFT, :], plane0[SHIFT:P, :].bitcast(I32))
         planes = [plane0[:], plane1[:].bitcast(U8)]
-        ts_psum = spread("ts", ts_turned)
+
+        ts_wide = spread("ts", ts_turned)
+        pr_wide = spread("pr", pr_turned)
 
         k_codes = keep.tile([P, PASSES, N], U16, name="k_codes", align_bytes=64)
         words = []
-
-        def gather_words(a):
-            w = keep.tile([P, PART], U32, name="words%d" % a, tag="words%d" % a, align_bytes=64)
-            nc.vector.tensor_copy(w[:], word_pool[:].bitcast(U32).indirect(offsets[:, a * PART // 16 : (a + 1) * PART // 16]))
-            words.append(w)
-
-        gather_words(0)
-        pr_wide = spread("pr", pr_turned)
-        gather_words(1)
         for a in range(PARTS):
-            nc.vector.tensor_copy(
-                k_codes[:, :, a * PART : (a + 1) * PART], words[a][:].bitcast(U16).rearrange("p (n o) -> p o n", o=PASSES)
-            )
+            gathered = keep.tile([P, PART], U32, name="words%d" % a, tag="words%d" % a, align_bytes=64)
+            entries = offsets[:, a * PART // GROUP : (a + 1) * PART // GROUP]
+            nc.vector.tensor_copy(gathered[:], word_pool[:].bitcast(U32).indirect(entries))
+            words.append(gathered)
+        for a in range(PARTS):
+            pairs = words[a][:].bitcast(U16).rearrange("p (n o) -> p o n", o=PASSES)
+            nc.vector.tensor_copy(k_codes[:, :, a * PART : (a + 1) * PART], pairs)
 
-        acc = [psum.tile([P, N], F32, name="acc%d" % h) for h in range(HALVES)]
-        grouped = {}
+        grouped00 = keep.tile([P, P, PACK], BF16, name="grouped00", tag="grouped00", align_bytes=64)
+        grouped01 = keep.tile([P, P, PACK], BF16, name="grouped01", align_bytes=64)
+        grouped1 = keep.tile([P, HALVES, P, PACK], BF16, name="grouped1", tag="grouped00", align_bytes=64)
+        grouped = {(0, 0): grouped00[:], (0, 1): grouped01[:], (1, 0): grouped1[:, 0], (1, 1): grouped1[:, 1]}
+        scores = [psum.tile([P, N], F32, name="scores%d" % h) for h in range(HALVES)]
 
-        def interleave(o, h, copy, tag):
-            g = keep.tile([P, P, PACK], BF16, name="grouped%d%d" % (o, h), tag=tag, align_bytes=64)
-            copy(g[:], q_raw[o][:, :, h * P : (h + 1) * P].rearrange("p j w -> p w j"))
-            grouped[o, h] = g
+        def interleave(o, h, copy):
+            copy(grouped[o, h], q_raw[o][:, :, h * P : (h + 1) * P].rearrange("p t q -> p q t"))
 
         def score(o, h, tag):
             codes = keep.tile([P, P], U32, name="q_codes%d%d" % (o, h), tag=tag, align_bytes=64)
             scales = keep.tile([P, P], U8, name="q_scales%d%d" % (o, h), align_bytes=64)
-            nc.vector.quantize_mx(out=codes[:].bitcast(FP8X4), scales=scales[:], in_=grouped[o, h][:].rearrange("p w j -> p (w j)"))
+            flat = grouped[o, h].rearrange("p q t -> p (q t)")
+            nc.vector.quantize_mx(out=codes[:].bitcast(FP8X4), scales=scales[:], in_=flat)
             nc.tensor.matmul_mx(
-                out=acc[h][:],
+                out=scores[h][:],
                 lhsT=codes[:].bitcast(FP8X4),
                 lhsT_scale=scales[:],
                 rhs=k_codes[:, o, :].bitcast(FP4X4),
@@ -125,26 +126,26 @@ def tile_attend_sigprior_srt_kernel(tc, qT, k_words, k_scales, ts, pr, offs, out
                 stop=(o == PASSES - 1),
             )
 
-        interleave(0, 0, nc.scalar.copy, "grouped00")
-        interleave(0, 1, nc.scalar.copy, "grouped01")
-        interleave(1, 1, nc.scalar.copy, "grouped11")
-        ts_wide = keep.tile([P, N], F32, name="ts_wide_sb", align_bytes=64)
-        nc.scalar.copy(ts_wide[:], ts_psum[:])
+        interleave(0, 0, nc.scalar.copy)
+        interleave(0, 1, nc.scalar.copy)
+        ts_sbuf = keep.tile([P, N], F32, name="ts_sbuf", tag="q_raw0", align_bytes=64)
+        nc.scalar.copy(ts_sbuf[:], ts_wide[:])
         score(0, 0, "words0")
-        interleave(1, 0, nc.vector.tensor_copy, "words1")
-        score(0, 1, "grouped00")
+        interleave(1, 0, nc.vector.tensor_copy)
+        score(0, 1, "words1")
         score(1, 0, "codes10")
-        score(1, 1, "words1")
+        interleave(1, 1, nc.vector.tensor_copy)
+        score(1, 1, "codes11")
 
         pieces = [(h, slice(a * PART, (a + 1) * PART)) for h in range(HALVES) for a in range(PARTS)]
         gates = []
-        for i, (h, cols) in enumerate(pieces):
-            s = keep.tile([P, PART], F32, name="scaled%d" % i, align_bytes=64)
-            nc.vector.tensor_tensor(s[:], acc[h][:, cols], ts_wide[:, cols], MULT)
-            g = keep.tile([P, PART], F32, name="gate%d" % i, align_bytes=64)
-            nc.scalar.activation(g[:], s[:], SIGMOID)
-            gates.append(g)
-        for i, (h, cols) in enumerate(pieces):
-            res = keep.tile([P, PART], F32, name="result%d" % i, align_bytes=64)
-            nc.vector.tensor_tensor(res[:], gates[i][:], pr_wide[:, cols], MULT)
-            nc.sync.dma_start(out[0, h * P : (h + 1) * P, cols], res[:])
+        for i, (h, slots) in enumerate(pieces):
+            scaled = keep.tile([P, PART], F32, name="scaled%d" % i, align_bytes=64)
+            nc.vector.tensor_tensor(scaled[:], scores[h][:, slots], ts_sbuf[:, slots], MULT)
+            gate = keep.tile([P, PART], F32, name="gate%d" % i, align_bytes=64)
+            nc.scalar.activation(gate[:], scaled[:], SIGMOID)
+            gates.append(gate)
+        for i, (h, slots) in enumerate(pieces):
+            result = keep.tile([P, PART], F32, name="result%d" % i, align_bytes=64)
+            nc.vector.tensor_tensor(result[:], gates[i][:], pr_wide[:, slots], MULT)
+            nc.sync.dma_start(out[0, h * P : (h + 1) * P, slots], result[:])

@@ -15,7 +15,9 @@ U8 = mybir.dt.uint8
 FP8X4 = mybir.dt.float8_e4m3fn_x4
 FP4X4 = mybir.dt.float4_e2m1fn_x4
 MULT = mybir.AluOpType.mult
-SIGMOID = mybir.ActivationFunctionType.Sigmoid
+ADD = mybir.AluOpType.add
+TANH = mybir.ActivationFunctionType.Tanh
+COPY = mybir.ActivationFunctionType.Copy
 
 P = 128
 PACK = 4
@@ -28,6 +30,8 @@ ROW = P - 1
 SHIFT = 16
 PARTS = 2
 PART = N // PARTS
+RUN = T // P
+BANK = 4
 
 
 def tile_attend_sigprior_srt_kernel(tc, qT, k_words, k_scales, ts, pr, offs, out):
@@ -45,13 +49,13 @@ def tile_attend_sigprior_srt_kernel(tc, qT, k_words, k_scales, ts, pr, offs, out
         ident = keep.tile([P, P], F32, name="ident", align_bytes=64)
 
         nc.vector.memset(scale_pool[:], 0)
-        nc.vector.memset(ts_pool[0:ROW, :], 0.0)
         nc.vector.memset(pr_pool[0:ROW, :], 0.0)
         nc.vector.memset(plane1[:], 0)
         make_identity(nc, ident[:])
 
         nc.sync.dma_start(offsets[:], offs)
-        nc.sync.dma_start(ts_pool[ROW:P, :], ts[0:1, :])
+        ts_runs = keep.tile([P, RUN], F32, name="ts_runs", align_bytes=64)
+        nc.sync.dma_start(ts_runs[:], ts[0].rearrange("(p j) -> p j", j=RUN))
         nc.sync.dma_start(pr_pool[ROW:P, :], pr[0:1, :])
         scale_rows = k_scales.bitcast(I32).rearrange("o (g r) t -> r g o t", r=SCALE_ROWS)
         for r in range(SCALE_ROWS):
@@ -64,32 +68,29 @@ def tile_attend_sigprior_srt_kernel(tc, qT, k_words, k_scales, ts, pr, offs, out
             nc.sync.dma_start(raw[:], rows.rearrange("(p t) q -> p t q", t=PACK))
             q_raw.append(raw)
 
-        def pick_and_turn(name, pool):
-            picked = keep.tile([P, N], F32, name=name + "_picked", align_bytes=64)
-            nc.vector.tensor_copy(picked[:], pool[:].indirect(offsets[:]))
-            turned = psum.tile([P, BLOCKS, P], F32, name=name + "_turned")
-            for j in range(BLOCKS):
-                nc.tensor.transpose(turned[:, j, :], picked[:, j * P : (j + 1) * P], ident[:])
-            return turned
-
-        def spread(name, turned):
-            cols = keep.tile([P, BLOCKS], F32, name=name + "_cols", align_bytes=64)
-            nc.scalar.copy(cols[:], turned[:, :, ROW])
-            wide = psum.tile([P, N], F32, name=name + "_wide")
-            for j in range(BLOCKS):
-                nc.tensor.transpose(wide[:, j * P : (j + 1) * P], cols[:, j : j + 1].to_broadcast([P, P]), ident[:])
-            return wide
-
-        ts_turned = pick_and_turn("ts", ts_pool)
-        pr_turned = pick_and_turn("pr", pr_pool)
+        ts_tokens = ts_pool[:].rearrange("m (p j) -> m p j", j=RUN)
+        for b in range(RUN // BANK):
+            bank = psum.tile([P, BANK, P], F32, name="ts_bank%d" % b)
+            for j in range(BANK):
+                column = ts_runs[:, b * BANK + j : b * BANK + j + 1]
+                nc.tensor.transpose(bank[:, j, :], column.to_broadcast([P, P]), ident[:])
+            nc.scalar.copy(ts_tokens[:, :, b * BANK : (b + 1) * BANK], bank[:].rearrange("m j p -> m p j"))
 
         plane0 = keep.tile([P, N], U8, name="plane0", align_bytes=64)
         nc.vector.tensor_copy(plane0[:], scale_pool[:].bitcast(U8).indirect(offsets[:]))
         nc.sync.dma_start(plane1[0 : P - SHIFT, :], plane0[SHIFT:P, :].bitcast(I32))
         planes = [plane0[:], plane1[:].bitcast(U8)]
 
-        ts_wide = spread("ts", ts_turned)
-        pr_wide = spread("pr", pr_turned)
+        picked = keep.tile([P, N], F32, name="picked", align_bytes=64)
+        nc.vector.tensor_copy(picked[:], pr_pool[:].indirect(offsets[:]))
+        turned = psum.tile([P, BLOCKS, P], F32, name="turned")
+        for j in range(BLOCKS):
+            nc.tensor.transpose(turned[:, j, :], picked[:, j * P : (j + 1) * P], ident[:])
+        cols = keep.tile([P, BLOCKS], F32, name="cols", align_bytes=64)
+        nc.scalar.activation(cols[:], turned[:, :, ROW], COPY, scale=0.5)
+        half_pr = psum.tile([P, N], F32, name="half_pr")
+        for j in range(BLOCKS):
+            nc.tensor.transpose(half_pr[:, j * P : (j + 1) * P], cols[:, j : j + 1].to_broadcast([P, P]), ident[:])
 
         k_codes = keep.tile([P, PASSES, N], U16, name="k_codes", align_bytes=64)
         words = []
@@ -102,14 +103,16 @@ def tile_attend_sigprior_srt_kernel(tc, qT, k_words, k_scales, ts, pr, offs, out
             pairs = words[a][:].bitcast(U16).rearrange("p (n o) -> p o n", o=PASSES)
             nc.vector.tensor_copy(k_codes[:, :, a * PART : (a + 1) * PART], pairs)
 
-        grouped00 = keep.tile([P, P, PACK], BF16, name="grouped00", tag="grouped00", align_bytes=64)
-        grouped01 = keep.tile([P, P, PACK], BF16, name="grouped01", align_bytes=64)
-        grouped1 = keep.tile([P, HALVES, P, PACK], BF16, name="grouped1", tag="grouped00", align_bytes=64)
-        grouped = {(0, 0): grouped00[:], (0, 1): grouped01[:], (1, 0): grouped1[:, 0], (1, 1): grouped1[:, 1]}
+        grouped = {}
+        for o in range(PASSES):
+            for h in range(HALVES):
+                name = "grouped%d%d" % (o, h)
+                grouped[o, h] = keep.tile([P, P, PACK], BF16, name=name, tag=name, align_bytes=64)[:]
         scores = [psum.tile([P, N], F32, name="scores%d" % h) for h in range(HALVES)]
 
         def interleave(o, h, copy):
-            copy(grouped[o, h], q_raw[o][:, :, h * P : (h + 1) * P].rearrange("p t q -> p q t"))
+            rows = q_raw[o][:, :, h * P : (h + 1) * P].rearrange("p t (c i) -> p c t i", i=PACK)
+            copy(grouped[o, h].rearrange("p (c i) t -> p c t i", i=PACK), rows)
 
         def score(o, h, tag):
             codes = keep.tile([P, P], U32, name="q_codes%d%d" % (o, h), tag=tag, align_bytes=64)
@@ -126,26 +129,32 @@ def tile_attend_sigprior_srt_kernel(tc, qT, k_words, k_scales, ts, pr, offs, out
                 stop=(o == PASSES - 1),
             )
 
-        interleave(0, 0, nc.scalar.copy)
-        interleave(0, 1, nc.scalar.copy)
-        ts_sbuf = keep.tile([P, N], F32, name="ts_sbuf", tag="q_raw0", align_bytes=64)
-        nc.scalar.copy(ts_sbuf[:], ts_wide[:])
+        def pick_ts(a):
+            part = keep.tile([P, PART], F32, name="ts_part%d" % a, tag="grouped0%d" % a, align_bytes=64)
+            entries = offsets[:, a * PART // GROUP : (a + 1) * PART // GROUP]
+            nc.vector.tensor_copy(part[:], ts_pool[:].indirect(entries))
+            return part
+
+        for o in range(PASSES):
+            for h in range(HALVES):
+                interleave(o, h, nc.scalar.copy)
         score(0, 0, "words0")
-        interleave(1, 0, nc.vector.tensor_copy)
+        ts_parts = [pick_ts(0)]
         score(0, 1, "words1")
+        ts_parts.append(pick_ts(1))
         score(1, 0, "codes10")
-        interleave(1, 1, nc.vector.tensor_copy)
         score(1, 1, "codes11")
 
-        pieces = [(h, slice(a * PART, (a + 1) * PART)) for h in range(HALVES) for a in range(PARTS)]
+        pieces = [(h, a) for h in range(HALVES) for a in range(PARTS)]
         gates = []
-        for i, (h, slots) in enumerate(pieces):
+        for i, (h, a) in enumerate(pieces):
             scaled = keep.tile([P, PART], F32, name="scaled%d" % i, align_bytes=64)
-            nc.vector.tensor_tensor(scaled[:], scores[h][:, slots], ts_sbuf[:, slots], MULT)
+            nc.vector.tensor_tensor(scaled[:], scores[h][:, a * PART : (a + 1) * PART], ts_parts[a][:], MULT)
             gate = keep.tile([P, PART], F32, name="gate%d" % i, align_bytes=64)
-            nc.scalar.activation(gate[:], scaled[:], SIGMOID)
+            nc.scalar.activation(gate[:], scaled[:], TANH, scale=0.5)
             gates.append(gate)
-        for i, (h, slots) in enumerate(pieces):
+        for i, (h, a) in enumerate(pieces):
+            slots = slice(a * PART, (a + 1) * PART)
             result = keep.tile([P, PART], F32, name="result%d" % i, align_bytes=64)
-            nc.vector.tensor_tensor(result[:], gates[i][:], pr_wide[:, slots], MULT)
+            nc.vector.scalar_tensor_tensor(result[:], gates[i][:], 1.0, half_pr[:, slots], op0=ADD, op1=MULT)
             nc.sync.dma_start(out[0, h * P : (h + 1) * P, slots], result[:])

@@ -41,25 +41,24 @@ def tile_attend_sigprior_srt_kernel(tc, qT, k_words, k_scales, ts, pr, offs, out
         psum = ctx.enter_context(tc.psum_pool(name="psum", bufs=1))
 
         offsets = keep.tile([P, N // GROUP], U16, name="offsets")
-        scale_pool = keep.tile([P, T // 4], I32, name="scale_pool", align_bytes=64)
+        scale_pool = keep.tile([P, T // 4], I32, name="scale_pool", tag="scale_pool", align_bytes=64)
         ts_pool = keep.tile([P, T], F32, name="ts_pool", align_bytes=64)
-        pr_pool = keep.tile([P, T], F32, name="pr_pool", align_bytes=64)
+        pr_pool = keep.tile([P, T], F32, name="pr_pool", tag="pr_pool", align_bytes=64)
         word_pool = keep.tile([P, T], I32, name="word_pool", align_bytes=64)
-        plane1 = keep.tile([P, N // 4], I32, name="plane1", align_bytes=64)
+        planes = keep.tile([P, PASSES, N // 4], I32, name="planes", align_bytes=64)
         ident = keep.tile([P, P], F32, name="ident", align_bytes=64)
 
-        nc.vector.memset(scale_pool[:], 0)
         nc.vector.memset(pr_pool[0:ROW, :], 0.0)
-        nc.vector.memset(plane1[:], 0)
+        nc.vector.memset(scale_pool[32:64, :], 0)
+        nc.vector.memset(scale_pool[64:P, :], 0)
+        nc.vector.memset(planes[:], 0)
         make_identity(nc, ident[:])
 
         nc.sync.dma_start(offsets[:], offs)
         ts_runs = keep.tile([P, RUN], F32, name="ts_runs", align_bytes=64)
-        nc.sync.dma_start(ts_runs[:], ts[0].rearrange("(p j) -> p j", j=RUN))
-        nc.sync.dma_start(pr_pool[ROW:P, :], pr[0:1, :])
-        scale_rows = k_scales.bitcast(I32).rearrange("o (g r) t -> r g o t", r=SCALE_ROWS)
-        for r in range(SCALE_ROWS):
-            nc.sync.dma_start(scale_pool[r:P:SHIFT, :], scale_rows[r])
+        nc.scalar.dma_start(ts_runs[:], ts[0].rearrange("(p j) -> p j", j=RUN))
+        nc.scalar.dma_start(pr_pool[ROW:P, :], pr[0:1, :])
+        nc.sync.dma_start(scale_pool[0:32, :], k_scales.bitcast(I32).rearrange("o f t -> f o t"))
         nc.sync.dma_start(word_pool[:], k_words[0].rearrange("p t b -> p (t b)").bitcast(I32))
         q_raw = []
         for o in range(PASSES):
@@ -70,20 +69,15 @@ def tile_attend_sigprior_srt_kernel(tc, qT, k_words, k_scales, ts, pr, offs, out
 
         ts_tokens = ts_pool[:].rearrange("m (p j) -> m p j", j=RUN)
         for b in range(RUN // BANK):
-            bank = psum.tile([P, BANK, P], F32, name="ts_bank%d" % b)
+            bank = psum.tile([P, BANK, P], F32, name="ts_bank%d" % b, tag="ts_bank%d" % b)
             for j in range(BANK):
                 column = ts_runs[:, b * BANK + j : b * BANK + j + 1]
                 nc.tensor.transpose(bank[:, j, :], column.to_broadcast([P, P]), ident[:])
             nc.scalar.copy(ts_tokens[:, :, b * BANK : (b + 1) * BANK], bank[:].rearrange("m j p -> m p j"))
 
-        plane0 = keep.tile([P, N], U8, name="plane0", align_bytes=64)
-        nc.vector.tensor_copy(plane0[:], scale_pool[:].bitcast(U8).indirect(offsets[:]))
-        nc.sync.dma_start(plane1[0 : P - SHIFT, :], plane0[SHIFT:P, :].bitcast(I32))
-        planes = [plane0[:], plane1[:].bitcast(U8)]
-
-        picked = keep.tile([P, N], F32, name="picked", align_bytes=64)
+        picked = keep.tile([P, N], F32, name="picked", tag="grouped00", align_bytes=64)
         nc.vector.tensor_copy(picked[:], pr_pool[:].indirect(offsets[:]))
-        turned = psum.tile([P, BLOCKS, P], F32, name="turned")
+        turned = psum.tile([P, BLOCKS, P], F32, name="turned", tag="ts_bank0")
         for j in range(BLOCKS):
             nc.tensor.transpose(turned[:, j, :], picked[:, j * P : (j + 1) * P], ident[:])
         cols = keep.tile([P, BLOCKS], F32, name="cols", align_bytes=64)
@@ -92,10 +86,15 @@ def tile_attend_sigprior_srt_kernel(tc, qT, k_words, k_scales, ts, pr, offs, out
         for j in range(BLOCKS):
             nc.tensor.transpose(half_pr[:, j * P : (j + 1) * P], cols[:, j : j + 1].to_broadcast([P, P]), ident[:])
 
+        picked_scales = keep.tile([P, N], U8, name="picked_scales", align_bytes=64)
+        nc.vector.tensor_copy(picked_scales[:], scale_pool[:].bitcast(U8).indirect(offsets[:]))
+        for g in range(4):
+            nc.sync.dma_start(planes[32 * g : 32 * g + 4], picked_scales[8 * g : 8 * g + 8, :].bitcast(I32))
+
         k_codes = keep.tile([P, PASSES, N], U16, name="k_codes", align_bytes=64)
         words = []
         for a in range(PARTS):
-            gathered = keep.tile([P, PART], U32, name="words%d" % a, tag="words%d" % a, align_bytes=64)
+            gathered = keep.tile([P, PART], U32, name="words%d" % a, tag=("pr_pool", "scale_pool")[a], align_bytes=64)
             entries = offsets[:, a * PART // GROUP : (a + 1) * PART // GROUP]
             nc.vector.tensor_copy(gathered[:], word_pool[:].bitcast(U32).indirect(entries))
             words.append(gathered)
@@ -124,7 +123,7 @@ def tile_attend_sigprior_srt_kernel(tc, qT, k_words, k_scales, ts, pr, offs, out
                 lhsT=codes[:].bitcast(FP8X4),
                 lhsT_scale=scales[:],
                 rhs=k_codes[:, o, :].bitcast(FP4X4),
-                rhs_scale=planes[o],
+                rhs_scale=planes[:, o, :].bitcast(U8),
                 start=(o == 0),
                 stop=(o == PASSES - 1),
             )
@@ -138,9 +137,9 @@ def tile_attend_sigprior_srt_kernel(tc, qT, k_words, k_scales, ts, pr, offs, out
         for o in range(PASSES):
             for h in range(HALVES):
                 interleave(o, h, nc.scalar.copy)
-        score(0, 0, "words0")
+        score(0, 0, "pr_pool")
         ts_parts = [pick_ts(0)]
-        score(0, 1, "words1")
+        score(0, 1, "scale_pool")
         ts_parts.append(pick_ts(1))
         score(1, 0, "codes10")
         score(1, 1, "codes11")
@@ -155,6 +154,6 @@ def tile_attend_sigprior_srt_kernel(tc, qT, k_words, k_scales, ts, pr, offs, out
             gates.append(gate)
         for i, (h, a) in enumerate(pieces):
             slots = slice(a * PART, (a + 1) * PART)
-            result = keep.tile([P, PART], F32, name="result%d" % i, align_bytes=64)
+            result = keep.tile([P, PART], F32, name="result%d" % i, tag=("grouped00", "grouped01", "grouped10", "grouped11")[i], align_bytes=64)
             nc.vector.scalar_tensor_tensor(result[:], gates[i][:], 1.0, half_pr[:, slots], op0=ADD, op1=MULT)
             nc.sync.dma_start(out[0, h * P : (h + 1) * P, slots], result[:])

@@ -48,24 +48,26 @@ def tile_attend_sigprior_srt_kernel(tc, qT, k_words, k_scales, ts, pr, offs, out
         planes = keep.tile([P, PASSES, N // 4], I32, name="planes", align_bytes=64)
         ident = keep.tile([P, P], F32, name="ident", align_bytes=64)
 
-        nc.vector.memset(pr_pool[0:ROW, :], 0.0)
         nc.vector.memset(scale_pool[32:64, :], 0)
         nc.vector.memset(scale_pool[64:P, :], 0)
         nc.vector.memset(planes[:], 0)
+        nc.vector.memset(pr_pool[0:ROW, :], 0.0)
         make_identity(nc, ident[:])
 
         nc.sync.dma_start(offsets[:], offs)
-        ts_runs = keep.tile([P, RUN], F32, name="ts_runs", align_bytes=64)
-        nc.scalar.dma_start(ts_runs[:], ts[0].rearrange("(p j) -> p j", j=RUN))
-        nc.scalar.dma_start(pr_pool[ROW:P, :], pr[0:1, :])
         nc.sync.dma_start(scale_pool[0:32, :], k_scales.bitcast(I32).rearrange("o f t -> f o t"))
+        ts_runs = keep.tile([P, RUN], F32, name="ts_runs", align_bytes=64)
+        nc.sync.dma_start(ts_runs[:], ts[0].rearrange("(p j) -> p j", j=RUN))
+        nc.sync.dma_start(pr_pool[ROW:P, :], pr[0:1, :])
         nc.sync.dma_start(word_pool[:], k_words[0].rearrange("p t b -> p (t b)").bitcast(I32))
-        q_raw = []
-        for o in range(PASSES):
-            raw = keep.tile([P, PACK, NQ], F32, name="q_raw%d" % o, tag="q_raw%d" % o, align_bytes=64)
+
+        def load_queries(o, tag):
+            raw = keep.tile([P, PACK, NQ], F32, name="q_raw%d" % o, tag=tag, align_bytes=64)
             rows = qT[0, o * P * PACK : (o + 1) * P * PACK, :]
             nc.sync.dma_start(raw[:], rows.rearrange("(p t) q -> p t q", t=PACK))
-            q_raw.append(raw)
+            return raw
+
+        q_raw = [load_queries(0, "q_raw0")]
 
         ts_tokens = ts_pool[:].rearrange("m (p j) -> m p j", j=RUN)
         for b in range(RUN // BANK):
@@ -74,6 +76,12 @@ def tile_attend_sigprior_srt_kernel(tc, qT, k_words, k_scales, ts, pr, offs, out
                 column = ts_runs[:, b * BANK + j : b * BANK + j + 1]
                 nc.tensor.transpose(bank[:, j, :], column.to_broadcast([P, P]), ident[:])
             nc.scalar.copy(ts_tokens[:, :, b * BANK : (b + 1) * BANK], bank[:].rearrange("m j p -> m p j"))
+
+        picked_scales = keep.tile([P, N], U8, name="picked_scales", align_bytes=64)
+        nc.vector.tensor_copy(picked_scales[:], scale_pool[:].bitcast(U8).indirect(offsets[:]))
+        for g in range(4):
+            nc.sync.dma_start(planes[32 * g : 32 * g + 4], picked_scales[8 * g : 8 * g + 8, :].bitcast(I32))
+        q_raw.append(load_queries(1, "scale_pool"))
 
         picked = keep.tile([P, N], F32, name="picked", tag="grouped00", align_bytes=64)
         nc.vector.tensor_copy(picked[:], pr_pool[:].indirect(offsets[:]))
@@ -86,15 +94,10 @@ def tile_attend_sigprior_srt_kernel(tc, qT, k_words, k_scales, ts, pr, offs, out
         for j in range(BLOCKS):
             nc.tensor.transpose(half_pr[:, j * P : (j + 1) * P], cols[:, j : j + 1].to_broadcast([P, P]), ident[:])
 
-        picked_scales = keep.tile([P, N], U8, name="picked_scales", align_bytes=64)
-        nc.vector.tensor_copy(picked_scales[:], scale_pool[:].bitcast(U8).indirect(offsets[:]))
-        for g in range(4):
-            nc.sync.dma_start(planes[32 * g : 32 * g + 4], picked_scales[8 * g : 8 * g + 8, :].bitcast(I32))
-
         k_codes = keep.tile([P, PASSES, N], U16, name="k_codes", align_bytes=64)
         words = []
         for a in range(PARTS):
-            gathered = keep.tile([P, PART], U32, name="words%d" % a, tag=("pr_pool", "scale_pool")[a], align_bytes=64)
+            gathered = keep.tile([P, PART], U32, name="words%d" % a, tag=("words0", "pr_pool")[a], align_bytes=64)
             entries = offsets[:, a * PART // GROUP : (a + 1) * PART // GROUP]
             nc.vector.tensor_copy(gathered[:], word_pool[:].bitcast(U32).indirect(entries))
             words.append(gathered)
@@ -137,9 +140,9 @@ def tile_attend_sigprior_srt_kernel(tc, qT, k_words, k_scales, ts, pr, offs, out
         for o in range(PASSES):
             for h in range(HALVES):
                 interleave(o, h, nc.scalar.copy)
-        score(0, 0, "pr_pool")
+        score(0, 0, "words0")
         ts_parts = [pick_ts(0)]
-        score(0, 1, "scale_pool")
+        score(0, 1, "pr_pool")
         ts_parts.append(pick_ts(1))
         score(1, 0, "codes10")
         score(1, 1, "codes11")

@@ -38,24 +38,26 @@ def tile_attend_sigprior_srt_kernel(tc, qT, k_words, k_scales, ts, pr, offs, out
     nc = tc.nc
     with ExitStack() as ctx:
         keep = ctx.enter_context(tc.tile_pool(name="keep", bufs=1))
+        shared = ctx.enter_context(tc.tile_pool(name="shared", bufs=1))
         psum = ctx.enter_context(tc.psum_pool(name="psum", bufs=1))
 
         offsets = keep.tile([P, N // GROUP], U16, name="offsets")
-        scale_pool = keep.tile([P, T // 4], I32, name="scale_pool", tag="scale_pool", align_bytes=64)
+        scale_pool = keep.tile([P, T // 4 + 8], I32, name="scale_pool", tag="scale_pool", align_bytes=64)
         ts_pool = keep.tile([P, T], F32, name="ts_pool", align_bytes=64)
-        pr_pool = keep.tile([P, T], F32, name="pr_pool", tag="pr_pool", align_bytes=64)
+        pr_pool = shared.tile([P, T], F32, name="pr_pool", align_bytes=64, offset=0)
         word_pool = keep.tile([P, T], I32, name="word_pool", align_bytes=64)
-        planes = keep.tile([P, PASSES, N // 4], I32, name="planes", align_bytes=64)
+        planes = keep.tile([P, PASSES * N // 4 + 8], I32, name="planes", align_bytes=64)
         ident = keep.tile([P, P], F32, name="ident", align_bytes=64)
 
-        nc.vector.memset(scale_pool[32:64, :], 0)
-        nc.vector.memset(scale_pool[64:P, :], 0)
-        nc.vector.memset(planes[:], 0)
-        nc.vector.memset(pr_pool[0:ROW, :], 0.0)
+        nc.vector.memset(scale_pool[32:64, 0 : T // 4 + 1], 0)
+        nc.vector.memset(scale_pool[64:P, 0 : T // 4 + 1], 0)
+        nc.vector.memset(planes[:, 0 : PASSES * N // 4 + 1], 0)
         make_identity(nc, ident[:])
+        nc.gpsimd.memset(pr_pool[0:ROW, 0:P], 0.0)
+        nc.gpsimd.memset(pr_pool[0:ROW, P:T], 0.0)
 
         nc.sync.dma_start(offsets[:], offs)
-        nc.sync.dma_start(scale_pool[0:32, :], k_scales.bitcast(I32).rearrange("o f t -> f o t"))
+        nc.sync.dma_start(scale_pool[0:32, 0 : T // 4], k_scales.bitcast(I32).rearrange("o f t -> f o t"))
         ts_runs = keep.tile([P, RUN], F32, name="ts_runs", align_bytes=64)
         nc.sync.dma_start(ts_runs[:], ts[0].rearrange("(p j) -> p j", j=RUN))
         nc.sync.dma_start(pr_pool[ROW:P, :], pr[0:1, :])
@@ -78,9 +80,9 @@ def tile_attend_sigprior_srt_kernel(tc, qT, k_words, k_scales, ts, pr, offs, out
             nc.scalar.copy(ts_tokens[:, :, b * BANK : (b + 1) * BANK], bank[:].rearrange("m j p -> m p j"))
 
         picked_scales = keep.tile([P, N], U8, name="picked_scales", align_bytes=64)
-        nc.vector.tensor_copy(picked_scales[:], scale_pool[:].bitcast(U8).indirect(offsets[:]))
+        nc.vector.tensor_copy(picked_scales[:], scale_pool[:, 0 : T // 4].bitcast(U8).indirect(offsets[:]))
         for g in range(4):
-            nc.sync.dma_start(planes[32 * g : 32 * g + 4], picked_scales[8 * g : 8 * g + 8, :].bitcast(I32))
+            nc.sync.dma_start(planes[32 * g : 32 * g + 4, 0 : PASSES * N // 4], picked_scales[8 * g : 8 * g + 8, :].bitcast(I32))
         q_raw.append(load_queries(1, "scale_pool"))
 
         picked = keep.tile([P, N], F32, name="picked", tag="grouped00", align_bytes=64)
@@ -97,7 +99,7 @@ def tile_attend_sigprior_srt_kernel(tc, qT, k_words, k_scales, ts, pr, offs, out
         k_codes = keep.tile([P, PASSES, N], U16, name="k_codes", align_bytes=64)
         words = []
         for a in range(PARTS):
-            gathered = keep.tile([P, PART], U32, name="words%d" % a, tag=("words0", "pr_pool")[a], align_bytes=64)
+            gathered = shared.tile([P, PART], U32, name="words%d" % a, align_bytes=64, offset=4 * PART * a)
             entries = offsets[:, a * PART // GROUP : (a + 1) * PART // GROUP]
             nc.vector.tensor_copy(gathered[:], word_pool[:].bitcast(U32).indirect(entries))
             words.append(gathered)
@@ -116,8 +118,12 @@ def tile_attend_sigprior_srt_kernel(tc, qT, k_words, k_scales, ts, pr, offs, out
             rows = q_raw[o][:, :, h * P : (h + 1) * P].rearrange("p t (c i) -> p c t i", i=PACK)
             copy(grouped[o, h].rearrange("p (c i) t -> p c t i", i=PACK), rows)
 
-        def score(o, h, tag):
-            codes = keep.tile([P, P], U32, name="q_codes%d%d" % (o, h), tag=tag, align_bytes=64)
+        def score(o, h):
+            name = "q_codes%d%d" % (o, h)
+            if o == 0:
+                codes = shared.tile([P, P], U32, name=name, align_bytes=64, offset=4 * PART * h)
+            else:
+                codes = keep.tile([P, P], U32, name=name, align_bytes=64)
             scales = keep.tile([P, P], U8, name="q_scales%d%d" % (o, h), align_bytes=64)
             flat = grouped[o, h].rearrange("p q t -> p (q t)")
             nc.vector.quantize_mx(out=codes[:].bitcast(FP8X4), scales=scales[:], in_=flat)
@@ -126,13 +132,13 @@ def tile_attend_sigprior_srt_kernel(tc, qT, k_words, k_scales, ts, pr, offs, out
                 lhsT=codes[:].bitcast(FP8X4),
                 lhsT_scale=scales[:],
                 rhs=k_codes[:, o, :].bitcast(FP4X4),
-                rhs_scale=planes[:, o, :].bitcast(U8),
+                rhs_scale=planes[:, o * N // 4 : (o + 1) * N // 4].bitcast(U8),
                 start=(o == 0),
                 stop=(o == PASSES - 1),
             )
 
         def pick_ts(a):
-            part = keep.tile([P, PART], F32, name="ts_part%d" % a, tag="grouped0%d" % a, align_bytes=64)
+            part = keep.tile([P, PART], F32, name="ts_part%d" % a, tag=("q_raw0", "scale_pool")[a], align_bytes=64)
             entries = offsets[:, a * PART // GROUP : (a + 1) * PART // GROUP]
             nc.vector.tensor_copy(part[:], ts_pool[:].indirect(entries))
             return part
@@ -140,12 +146,12 @@ def tile_attend_sigprior_srt_kernel(tc, qT, k_words, k_scales, ts, pr, offs, out
         for o in range(PASSES):
             for h in range(HALVES):
                 interleave(o, h, nc.scalar.copy)
-        score(0, 0, "words0")
+        score(0, 0)
+        score(0, 1)
         ts_parts = [pick_ts(0)]
-        score(0, 1, "pr_pool")
+        score(1, 0)
+        score(1, 1)
         ts_parts.append(pick_ts(1))
-        score(1, 0, "codes10")
-        score(1, 1, "codes11")
 
         pieces = [(h, a) for h in range(HALVES) for a in range(PARTS)]
         gates = []
@@ -157,6 +163,6 @@ def tile_attend_sigprior_srt_kernel(tc, qT, k_words, k_scales, ts, pr, offs, out
             gates.append(gate)
         for i, (h, a) in enumerate(pieces):
             slots = slice(a * PART, (a + 1) * PART)
-            result = keep.tile([P, PART], F32, name="result%d" % i, tag=("grouped00", "grouped01", "grouped10", "grouped11")[i], align_bytes=64)
+            result = keep.tile([P, PART], F32, name="result%d" % i, tag=("q_raw0", "scale_pool", "grouped10", "grouped11")[i], align_bytes=64)
             nc.vector.scalar_tensor_tensor(result[:], gates[i][:], 1.0, half_pr[:, slots], op0=ADD, op1=MULT)
             nc.sync.dma_start(out[0, h * P : (h + 1) * P, slots], result[:])

@@ -61,7 +61,6 @@ def tile_attend_sigprior_srt_kernel(tc, qT, k_words, k_scales, ts, pr, offs, out
         ts_runs = keep.tile([P, RUN], F32, name="ts_runs", align_bytes=64)
         nc.sync.dma_start(ts_runs[:], ts[0].rearrange("(p j) -> p j", j=RUN))
         nc.sync.dma_start(pr_pool[ROW:P, :], pr[0:1, :])
-        nc.sync.dma_start(word_pool[:], k_words[0].rearrange("p t b -> p (t b)").bitcast(I32))
 
         def load_queries(o, tag):
             raw = keep.tile([P, PACK, NQ], F32, name="q_raw%d" % o, tag=tag, align_bytes=64)
@@ -70,6 +69,7 @@ def tile_attend_sigprior_srt_kernel(tc, qT, k_words, k_scales, ts, pr, offs, out
             return raw
 
         q_raw = [load_queries(0, "q_raw0")]
+        nc.sync.dma_start(word_pool[:], k_words[0].rearrange("p t b -> p (t b)").bitcast(I32))
 
         ts_tokens = ts_pool[:].rearrange("m (p j) -> m p j", j=RUN)
         for b in range(RUN // BANK):
@@ -85,14 +85,14 @@ def tile_attend_sigprior_srt_kernel(tc, qT, k_words, k_scales, ts, pr, offs, out
             nc.sync.dma_start(planes[32 * g : 32 * g + 4, 0 : PASSES * N // 4], picked_scales[8 * g : 8 * g + 8, :].bitcast(I32))
         q_raw.append(load_queries(1, "scale_pool"))
 
-        picked = keep.tile([P, N], F32, name="picked", tag="grouped00", align_bytes=64)
+        picked = keep.tile([P, N], F32, name="picked", align_bytes=64)
         nc.vector.tensor_copy(picked[:], pr_pool[:].indirect(offsets[:]))
         turned = psum.tile([P, BLOCKS, P], F32, name="turned", tag="ts_bank0")
         for j in range(BLOCKS):
             nc.tensor.transpose(turned[:, j, :], picked[:, j * P : (j + 1) * P], ident[:])
         cols = keep.tile([P, BLOCKS], F32, name="cols", align_bytes=64)
         nc.scalar.activation(cols[:], turned[:, :, ROW], COPY, scale=0.5)
-        half_pr = psum.tile([P, N], F32, name="half_pr")
+        half_pr = psum.tile([P, N], F32, name="half_pr", tag="ts_bank1")
         for j in range(BLOCKS):
             nc.tensor.transpose(half_pr[:, j * P : (j + 1) * P], cols[:, j : j + 1].to_broadcast([P, P]), ident[:])
 
@@ -112,7 +112,10 @@ def tile_attend_sigprior_srt_kernel(tc, qT, k_words, k_scales, ts, pr, offs, out
             for h in range(HALVES):
                 name = "grouped%d%d" % (o, h)
                 grouped[o, h] = keep.tile([P, P, PACK], BF16, name=name, tag=name, align_bytes=64)[:]
-        scores = [psum.tile([P, N], F32, name="scores%d" % h) for h in range(HALVES)]
+        scores = {}
+        for h in range(HALVES):
+            for a in range(PARTS):
+                scores[h, a] = psum.tile([P, PART], F32, name="scores%d%d" % (h, a))
 
         def interleave(o, h, copy):
             rows = q_raw[o][:, :, h * P : (h + 1) * P].rearrange("p t (c i) -> p c t i", i=PACK)
@@ -120,49 +123,54 @@ def tile_attend_sigprior_srt_kernel(tc, qT, k_words, k_scales, ts, pr, offs, out
 
         def score(o, h):
             name = "q_codes%d%d" % (o, h)
-            if o == 0:
-                codes = shared.tile([P, P], U32, name=name, align_bytes=64, offset=4 * PART * h)
+            if (o, h) == (0, 1):
+                codes = shared.tile([P, P], U32, name=name, align_bytes=64, offset=0)
             else:
                 codes = keep.tile([P, P], U32, name=name, align_bytes=64)
             scales = keep.tile([P, P], U8, name="q_scales%d%d" % (o, h), align_bytes=64)
             flat = grouped[o, h].rearrange("p q t -> p (q t)")
             nc.vector.quantize_mx(out=codes[:].bitcast(FP8X4), scales=scales[:], in_=flat)
-            nc.tensor.matmul_mx(
-                out=scores[h][:],
-                lhsT=codes[:].bitcast(FP8X4),
-                lhsT_scale=scales[:],
-                rhs=k_codes[:, o, :].bitcast(FP4X4),
-                rhs_scale=planes[:, o * N // 4 : (o + 1) * N // 4].bitcast(U8),
-                start=(o == 0),
-                stop=(o == PASSES - 1),
-            )
+            for a in range(PARTS):
+                first = (o * N + a * PART) // 4
+                nc.tensor.matmul_mx(
+                    out=scores[h, a][:],
+                    lhsT=codes[:].bitcast(FP8X4),
+                    lhsT_scale=scales[:],
+                    rhs=k_codes[:, o, a * PART : (a + 1) * PART].bitcast(FP4X4),
+                    rhs_scale=planes[:, first : first + PART // 4].bitcast(U8),
+                    start=(o == 0),
+                    stop=(o == PASSES - 1),
+                )
 
         def pick_ts(a):
-            part = keep.tile([P, PART], F32, name="ts_part%d" % a, tag=("q_raw0", "scale_pool")[a], align_bytes=64)
+            part = keep.tile([P, PART], F32, name="ts_part%d" % a, align_bytes=64)
             entries = offsets[:, a * PART // GROUP : (a + 1) * PART // GROUP]
-            nc.vector.tensor_copy(part[:], ts_pool[:].indirect(entries))
+            if a == 0:
+                nc.vector.tensor_copy(part[:], ts_pool[:].indirect(entries))
+            else:
+                nc.scalar.activation(part[:], ts_pool[:].indirect(entries), COPY)
             return part
 
         for o in range(PASSES):
             for h in range(HALVES):
-                interleave(o, h, nc.scalar.copy)
+                interleave(o, h, nc.scalar.copy if o + h else nc.vector.tensor_copy)
         score(0, 0)
         score(0, 1)
         ts_parts = [pick_ts(0)]
         score(1, 0)
-        score(1, 1)
         ts_parts.append(pick_ts(1))
+        score(1, 1)
 
         pieces = [(h, a) for h in range(HALVES) for a in range(PARTS)]
         gates = []
         for i, (h, a) in enumerate(pieces):
             scaled = keep.tile([P, PART], F32, name="scaled%d" % i, align_bytes=64)
-            nc.vector.tensor_tensor(scaled[:], scores[h][:, a * PART : (a + 1) * PART], ts_parts[a][:], MULT)
+            nc.vector.tensor_tensor(scaled[:], scores[h, a][:], ts_parts[a][:], MULT)
             gate = keep.tile([P, PART], F32, name="gate%d" % i, align_bytes=64)
             nc.scalar.activation(gate[:], scaled[:], TANH, scale=0.5)
             gates.append(gate)
         for i, (h, a) in enumerate(pieces):
             slots = slice(a * PART, (a + 1) * PART)
-            result = keep.tile([P, PART], F32, name="result%d" % i, tag=("q_raw0", "scale_pool", "grouped10", "grouped11")[i], align_bytes=64)
+            result = keep.tile([P, PART], F32, name="result%d" % i, align_bytes=64)
             nc.vector.scalar_tensor_tensor(result[:], gates[i][:], 1.0, half_pr[:, slots], op0=ADD, op1=MULT)
             nc.sync.dma_start(out[0, h * P : (h + 1) * P, slots], result[:])

@@ -25,9 +25,10 @@ PASSES = D // (P * PACK)
 HALVES = NQ // P
 BLOCKS = N // P
 GROUP = 16
+QUADRANT = 32
 SCALE_ROWS = 4
+WORD = 4
 ROW = P - 1
-SHIFT = 16
 PARTS = 2
 PART = N // PARTS
 RUN = T // P
@@ -42,25 +43,24 @@ def tile_attend_sigprior_srt_kernel(tc, qT, k_words, k_scales, ts, pr, offs, out
         psum = ctx.enter_context(tc.psum_pool(name="psum", bufs=1))
 
         offsets = keep.tile([P, N // GROUP], U16, name="offsets")
-        scale_pool = keep.tile([P, T // 4 + 8], I32, name="scale_pool", tag="scale_pool", align_bytes=64)
+        scale_pool = keep.tile([P, T // WORD], I32, name="scale_pool", tag="scale_pool", align_bytes=64)
         ts_pool = keep.tile([P, T], F32, name="ts_pool", align_bytes=64)
         pr_pool = shared.tile([P, T], F32, name="pr_pool", align_bytes=64, offset=0)
         word_pool = keep.tile([P, T], I32, name="word_pool", align_bytes=64)
-        planes = keep.tile([P, PASSES * N // 4 + 8], I32, name="planes", align_bytes=64)
+        planes = keep.tile([P, PASSES * N // WORD], I32, name="planes", align_bytes=64)
         ident = keep.tile([P, P], F32, name="ident", align_bytes=64)
 
-        nc.vector.memset(scale_pool[32:64, 0 : T // 4 + 1], 0)
-        nc.vector.memset(scale_pool[64:P, 0 : T // 4 + 1], 0)
-        nc.vector.memset(planes[:, 0 : PASSES * N // 4 + 1], 0)
+        def zero(rows):
+            cut = rows.shape[1] // 2 + 1
+            nc.vector.memset(rows[:, :cut], 0)
+            nc.vector.memset(rows[:, cut:], 0)
+
+        zero(scale_pool[QUADRANT : 2 * QUADRANT, :])
+        zero(scale_pool[2 * QUADRANT : P, :])
+        zero(planes[:])
         make_identity(nc, ident[:])
         nc.gpsimd.memset(pr_pool[0:ROW, 0:P], 0.0)
         nc.gpsimd.memset(pr_pool[0:ROW, P:T], 0.0)
-
-        nc.sync.dma_start(offsets[:], offs)
-        nc.sync.dma_start(scale_pool[0:32, 0 : T // 4], k_scales.bitcast(I32).rearrange("o f t -> f o t"))
-        ts_runs = keep.tile([P, RUN], F32, name="ts_runs", align_bytes=64)
-        nc.sync.dma_start(ts_runs[:], ts[0].rearrange("(p j) -> p j", j=RUN))
-        nc.sync.dma_start(pr_pool[ROW:P, :], pr[0:1, :])
 
         def load_queries(o, tag):
             raw = keep.tile([P, PACK, NQ], F32, name="q_raw%d" % o, tag=tag, align_bytes=64)
@@ -68,6 +68,11 @@ def tile_attend_sigprior_srt_kernel(tc, qT, k_words, k_scales, ts, pr, offs, out
             nc.sync.dma_start(raw[:], rows.rearrange("(p t) q -> p t q", t=PACK))
             return raw
 
+        nc.sync.dma_start(offsets[:], offs)
+        nc.sync.dma_start(scale_pool[0:QUADRANT, :], k_scales.bitcast(I32).rearrange("o f t -> f o t"))
+        ts_runs = keep.tile([P, RUN], F32, name="ts_runs", align_bytes=64)
+        nc.sync.dma_start(ts_runs[:], ts[0].rearrange("(p j) -> p j", j=RUN))
+        nc.sync.dma_start(pr_pool[ROW:P, :], pr[0:1, :])
         q_raw = [load_queries(0, "q_raw0")]
         nc.sync.dma_start(word_pool[:], k_words[0].rearrange("p t b -> p (t b)").bitcast(I32))
 
@@ -80,16 +85,17 @@ def tile_attend_sigprior_srt_kernel(tc, qT, k_words, k_scales, ts, pr, offs, out
             nc.scalar.copy(ts_tokens[:, :, b * BANK : (b + 1) * BANK], bank[:].rearrange("m j p -> m p j"))
 
         picked_scales = keep.tile([P, N], U8, name="picked_scales", align_bytes=64)
-        nc.vector.tensor_copy(picked_scales[:], scale_pool[:, 0 : T // 4].bitcast(U8).indirect(offsets[:]))
-        for g in range(4):
-            nc.sync.dma_start(planes[32 * g : 32 * g + 4, 0 : PASSES * N // 4], picked_scales[8 * g : 8 * g + 8, :].bitcast(I32))
+        nc.vector.tensor_copy(picked_scales[:], scale_pool[:].bitcast(U8).indirect(offsets[:]))
+        for g in range(P // QUADRANT):
+            scale_rows = picked_scales[g * PASSES * SCALE_ROWS : (g + 1) * PASSES * SCALE_ROWS, :]
+            nc.sync.dma_start(planes[g * QUADRANT : g * QUADRANT + SCALE_ROWS, :], scale_rows.bitcast(I32))
         q_raw.append(load_queries(1, "scale_pool"))
 
-        picked = keep.tile([P, N], F32, name="picked", align_bytes=64)
-        nc.vector.tensor_copy(picked[:], pr_pool[:].indirect(offsets[:]))
+        picked_pr = keep.tile([P, N], F32, name="picked_pr", align_bytes=64)
+        nc.vector.tensor_copy(picked_pr[:], pr_pool[:].indirect(offsets[:]))
         turned = psum.tile([P, BLOCKS, P], F32, name="turned", tag="ts_bank0")
         for j in range(BLOCKS):
-            nc.tensor.transpose(turned[:, j, :], picked[:, j * P : (j + 1) * P], ident[:])
+            nc.tensor.transpose(turned[:, j, :], picked_pr[:, j * P : (j + 1) * P], ident[:])
         cols = keep.tile([P, BLOCKS], F32, name="cols", align_bytes=64)
         nc.scalar.activation(cols[:], turned[:, :, ROW], COPY, scale=0.5)
         half_pr = psum.tile([P, N], F32, name="half_pr", tag="ts_bank1")
@@ -99,7 +105,7 @@ def tile_attend_sigprior_srt_kernel(tc, qT, k_words, k_scales, ts, pr, offs, out
         k_codes = keep.tile([P, PASSES, N], U16, name="k_codes", align_bytes=64)
         words = []
         for a in range(PARTS):
-            gathered = shared.tile([P, PART], U32, name="words%d" % a, align_bytes=64, offset=4 * PART * a)
+            gathered = shared.tile([P, PART], U32, name="words%d" % a, align_bytes=64, offset=WORD * PART * a)
             entries = offsets[:, a * PART // GROUP : (a + 1) * PART // GROUP]
             nc.vector.tensor_copy(gathered[:], word_pool[:].bitcast(U32).indirect(entries))
             words.append(gathered)
@@ -111,7 +117,7 @@ def tile_attend_sigprior_srt_kernel(tc, qT, k_words, k_scales, ts, pr, offs, out
         for o in range(PASSES):
             for h in range(HALVES):
                 name = "grouped%d%d" % (o, h)
-                grouped[o, h] = keep.tile([P, P, PACK], BF16, name=name, tag=name, align_bytes=64)[:]
+                grouped[o, h] = keep.tile([P, P, PACK], BF16, name=name, align_bytes=64)[:]
         scores = {}
         for h in range(HALVES):
             for a in range(PARTS):
@@ -131,13 +137,13 @@ def tile_attend_sigprior_srt_kernel(tc, qT, k_words, k_scales, ts, pr, offs, out
             flat = grouped[o, h].rearrange("p q t -> p (q t)")
             nc.vector.quantize_mx(out=codes[:].bitcast(FP8X4), scales=scales[:], in_=flat)
             for a in range(PARTS):
-                first = (o * N + a * PART) // 4
+                first = (o * N + a * PART) // WORD
                 nc.tensor.matmul_mx(
                     out=scores[h, a][:],
                     lhsT=codes[:].bitcast(FP8X4),
                     lhsT_scale=scales[:],
                     rhs=k_codes[:, o, a * PART : (a + 1) * PART].bitcast(FP4X4),
-                    rhs_scale=planes[:, first : first + PART // 4].bitcast(U8),
+                    rhs_scale=planes[:, first : first + PART // WORD].bitcast(U8),
                     start=(o == 0),
                     stop=(o == PASSES - 1),
                 )
@@ -153,7 +159,7 @@ def tile_attend_sigprior_srt_kernel(tc, qT, k_words, k_scales, ts, pr, offs, out
 
         for o in range(PASSES):
             for h in range(HALVES):
-                interleave(o, h, nc.scalar.copy if o + h else nc.vector.tensor_copy)
+                interleave(o, h, nc.vector.tensor_copy if (o, h) == (0, 0) else nc.scalar.copy)
         score(0, 0)
         score(0, 1)
         ts_parts = [pick_ts(0)]

@@ -32,6 +32,7 @@ ROW = P - 1
 PARTS = 2
 PART = N // PARTS
 RUN = T // P
+PREFIX = T - N + PART
 BANK = 4
 
 
@@ -47,8 +48,8 @@ def tile_attend_sigprior_srt_kernel(tc, qT, k_words, k_scales, ts, pr, offs, out
         ts_pool = keep.tile([P, T], F32, name="ts_pool", align_bytes=64)
         pr_pool = shared.tile([P, T], F32, name="pr_pool", align_bytes=64, offset=0)
         word_pool = keep.tile([P, T], I32, name="word_pool", align_bytes=64)
-        planes = keep.tile([P, PASSES * N // WORD], I32, name="planes", align_bytes=64)
         ident = keep.tile([P, P], F32, name="ident", align_bytes=64)
+        first_ident = keep.tile([P, P], F32, name="first_ident", tag="planes", align_bytes=64)
 
         def zero(rows):
             cut = rows.shape[1] // 2 + 1
@@ -57,10 +58,9 @@ def tile_attend_sigprior_srt_kernel(tc, qT, k_words, k_scales, ts, pr, offs, out
 
         zero(scale_pool[QUADRANT : 2 * QUADRANT, :])
         zero(scale_pool[2 * QUADRANT : P, :])
-        zero(planes[:])
+        make_identity(nc, first_ident[:])
         make_identity(nc, ident[:])
-        nc.gpsimd.memset(pr_pool[0:ROW, 0:P], 0.0)
-        nc.gpsimd.memset(pr_pool[0:ROW, P:T], 0.0)
+        nc.gpsimd.memset(pr_pool[0:ROW, :], 0.0)
 
         def load_queries(o, tag):
             raw = keep.tile([P, PACK, NQ], F32, name="q_raw%d" % o, tag=tag, align_bytes=64)
@@ -68,28 +68,32 @@ def tile_attend_sigprior_srt_kernel(tc, qT, k_words, k_scales, ts, pr, offs, out
             nc.sync.dma_start(raw[:], rows.rearrange("(p t) q -> p t q", t=PACK))
             return raw
 
-        nc.sync.dma_start(offsets[:], offs)
-        nc.sync.dma_start(scale_pool[0:QUADRANT, :], k_scales.bitcast(I32).rearrange("o f t -> f o t"))
         ts_runs = keep.tile([P, RUN], F32, name="ts_runs", align_bytes=64)
         nc.sync.dma_start(ts_runs[:], ts[0].rearrange("(p j) -> p j", j=RUN))
+        nc.sync.dma_start(offsets[:], offs)
+        nc.sync.dma_start(scale_pool[0:QUADRANT, :], k_scales.bitcast(I32).rearrange("o f t -> f o t"))
         nc.sync.dma_start(pr_pool[ROW:P, :], pr[0:1, :])
         q_raw = [load_queries(0, "q_raw0")]
-        nc.sync.dma_start(word_pool[:], k_words[0].rearrange("p t b -> p (t b)").bitcast(I32))
+        all_words = k_words[0].rearrange("p t b -> p (t b)").bitcast(I32)
+        nc.sync.dma_start(word_pool[:, :PREFIX], all_words[:, :PREFIX])
+        nc.sync.dma_start(word_pool[:, PREFIX:], all_words[:, PREFIX:])
 
         ts_tokens = ts_pool[:].rearrange("m (p j) -> m p j", j=RUN)
         for b in range(RUN // BANK):
             bank = psum.tile([P, BANK, P], F32, name="ts_bank%d" % b, tag="ts_bank%d" % b)
             for j in range(BANK):
                 column = ts_runs[:, b * BANK + j : b * BANK + j + 1]
-                nc.tensor.transpose(bank[:, j, :], column.to_broadcast([P, P]), ident[:])
+                nc.tensor.transpose(bank[:, j, :], column.to_broadcast([P, P]), (first_ident if b < 2 else ident)[:])
             nc.scalar.copy(ts_tokens[:, :, b * BANK : (b + 1) * BANK], bank[:].rearrange("m j p -> m p j"))
 
+        planes = keep.tile([P, PASSES * N // WORD], I32, name="planes", tag="planes", align_bytes=64)
+        nc.gpsimd.memset(planes[:], 0)
         picked_scales = keep.tile([P, N], U8, name="picked_scales", align_bytes=64)
         nc.vector.tensor_copy(picked_scales[:], scale_pool[:].bitcast(U8).indirect(offsets[:]))
         for g in range(P // QUADRANT):
             scale_rows = picked_scales[g * PASSES * SCALE_ROWS : (g + 1) * PASSES * SCALE_ROWS, :]
-            nc.sync.dma_start(planes[g * QUADRANT : g * QUADRANT + SCALE_ROWS, :], scale_rows.bitcast(I32))
-        q_raw.append(load_queries(1, "scale_pool"))
+            nc.scalar.dma_start(planes[g * QUADRANT : g * QUADRANT + SCALE_ROWS, :], scale_rows.bitcast(I32))
+        q_raw.append(load_queries(1, "q_raw1"))
 
         picked_pr = keep.tile([P, N], F32, name="picked_pr", align_bytes=64)
         nc.vector.tensor_copy(picked_pr[:], pr_pool[:].indirect(offsets[:]))
@@ -107,7 +111,8 @@ def tile_attend_sigprior_srt_kernel(tc, qT, k_words, k_scales, ts, pr, offs, out
         for a in range(PARTS):
             gathered = shared.tile([P, PART], U32, name="words%d" % a, align_bytes=64, offset=WORD * PART * a)
             entries = offsets[:, a * PART // GROUP : (a + 1) * PART // GROUP]
-            nc.vector.tensor_copy(gathered[:], word_pool[:].bitcast(U32).indirect(entries))
+            window = word_pool[:, : T - N + (a + 1) * PART]
+            nc.vector.tensor_copy(gathered[:], window.bitcast(U32).indirect(entries))
             words.append(gathered)
         for a in range(PARTS):
             pairs = words[a][:].bitcast(U16).rearrange("p (n o) -> p o n", o=PASSES)
@@ -127,12 +132,12 @@ def tile_attend_sigprior_srt_kernel(tc, qT, k_words, k_scales, ts, pr, offs, out
             rows = q_raw[o][:, :, h * P : (h + 1) * P].rearrange("p t (c i) -> p c t i", i=PACK)
             copy(grouped[o, h].rearrange("p (c i) t -> p c t i", i=PACK), rows)
 
+        def round_on_gpsimd(to, rows):
+            nc.gpsimd.tensor_scalar(to, rows, 1.0, 0.0, op0=MULT, op1=ADD)
+
         def score(o, h):
             name = "q_codes%d%d" % (o, h)
-            if (o, h) == (0, 1):
-                codes = shared.tile([P, P], U32, name=name, align_bytes=64, offset=0)
-            else:
-                codes = keep.tile([P, P], U32, name=name, align_bytes=64)
+            codes = keep.tile([P, P], U32, name=name, align_bytes=64)
             scales = keep.tile([P, P], U8, name="q_scales%d%d" % (o, h), align_bytes=64)
             flat = grouped[o, h].rearrange("p q t -> p (q t)")
             nc.vector.quantize_mx(out=codes[:].bitcast(FP8X4), scales=scales[:], in_=flat)
@@ -149,23 +154,23 @@ def tile_attend_sigprior_srt_kernel(tc, qT, k_words, k_scales, ts, pr, offs, out
                 )
 
         def pick_ts(a):
-            part = keep.tile([P, PART], F32, name="ts_part%d" % a, align_bytes=64)
+            part = keep.tile([P, PART], F32, name="ts_part%d" % a, tag="q_raw1" if a else "ts_part0", align_bytes=64)
             entries = offsets[:, a * PART // GROUP : (a + 1) * PART // GROUP]
-            if a == 0:
-                nc.vector.tensor_copy(part[:], ts_pool[:].indirect(entries))
-            else:
-                nc.scalar.activation(part[:], ts_pool[:].indirect(entries), COPY)
+            nc.vector.tensor_copy(part[:], ts_pool[:].indirect(entries))
             return part
 
         for o in range(PASSES):
             for h in range(HALVES):
-                interleave(o, h, nc.vector.tensor_copy if (o, h) == (0, 0) else nc.scalar.copy)
+                if o == 0:
+                    round_on_gpsimd(grouped[o, h], q_raw[o][:, :, h * P : (h + 1) * P].rearrange("p t q -> p q t"))
+                else:
+                    interleave(o, h, nc.scalar.copy)
         score(0, 0)
         score(0, 1)
         ts_parts = [pick_ts(0)]
         score(1, 0)
-        ts_parts.append(pick_ts(1))
         score(1, 1)
+        ts_parts.append(pick_ts(1))
 
         pieces = [(h, a) for h in range(HALVES) for a in range(PARTS)]
         gates = []

@@ -95,7 +95,7 @@ def tile_attend_sigprior_srt_kernel(tc, qT, k_words, k_scales, ts, pr, offs, out
             nc.scalar.dma_start(planes[g * QUADRANT : g * QUADRANT + SCALE_ROWS, :], scale_rows.bitcast(I32))
         q_raw.append(load_queries(1, "q_raw1"))
 
-        picked_pr = keep.tile([P, N], F32, name="picked_pr", align_bytes=64)
+        picked_pr = shared.tile([P, N], F32, name="picked_pr", align_bytes=64, offset=WORD * T)
         nc.vector.tensor_copy(picked_pr[:], pr_pool[:].indirect(offsets[:]))
         turned = psum.tile([P, BLOCKS, P], F32, name="turned", tag="ts_bank0")
         for j in range(BLOCKS):
@@ -122,7 +122,11 @@ def tile_attend_sigprior_srt_kernel(tc, qT, k_words, k_scales, ts, pr, offs, out
         for o in range(PASSES):
             for h in range(HALVES):
                 name = "grouped%d%d" % (o, h)
-                grouped[o, h] = keep.tile([P, P, PACK], BF16, name=name, align_bytes=64)[:]
+                if o == 1:
+                    place = WORD * T + 2 * P * PACK * h
+                    grouped[o, h] = shared.tile([P, P, PACK], BF16, name=name, align_bytes=64, offset=place)[:]
+                else:
+                    grouped[o, h] = keep.tile([P, P, PACK], BF16, name=name, align_bytes=64)[:]
         scores = {}
         for h in range(HALVES):
             for a in range(PARTS):
@@ -154,11 +158,15 @@ def tile_attend_sigprior_srt_kernel(tc, qT, k_words, k_scales, ts, pr, offs, out
                 )
 
         def pick_ts(a):
-            part = keep.tile([P, PART], F32, name="ts_part%d" % a, tag="q_raw1" if a else "ts_part0", align_bytes=64)
+            part = keep.tile([P, PART], F32, name="ts_part%d" % a, align_bytes=64)
             entries = offsets[:, a * PART // GROUP : (a + 1) * PART // GROUP]
-            nc.vector.tensor_copy(part[:], ts_pool[:].indirect(entries))
+            if a == 0:
+                nc.scalar.activation(part[:], ts_pool[:].indirect(entries), COPY)
+            else:
+                nc.vector.tensor_copy(part[:], ts_pool[:].indirect(entries))
             return part
 
+        ts_parts = [pick_ts(0)]
         for o in range(PASSES):
             for h in range(HALVES):
                 if o == 0:
@@ -167,10 +175,9 @@ def tile_attend_sigprior_srt_kernel(tc, qT, k_words, k_scales, ts, pr, offs, out
                     interleave(o, h, nc.scalar.copy)
         score(0, 0)
         score(0, 1)
-        ts_parts = [pick_ts(0)]
+        ts_parts.append(pick_ts(1))
         score(1, 0)
         score(1, 1)
-        ts_parts.append(pick_ts(1))
 
         pieces = [(h, a) for h in range(HALVES) for a in range(PARTS)]
         gates = []

@@ -46,10 +46,10 @@ def tile_attend_sigprior_srt_kernel(tc, qT, k_words, k_scales, ts, pr, offs, out
         offsets = keep.tile([P, N // GROUP], U16, name="offsets")
         scale_pool = keep.tile([P, T // WORD], I32, name="scale_pool", tag="scale_pool", align_bytes=64)
         ts_pool = keep.tile([P, T], F32, name="ts_pool", align_bytes=64)
-        pr_pool = shared.tile([P, T], F32, name="pr_pool", align_bytes=64, offset=0)
+        pr_pool = keep.tile([P, T], F32, name="pr_pool", align_bytes=64)
         word_pool = keep.tile([P, T], I32, name="word_pool", align_bytes=64)
         ident = keep.tile([P, P], F32, name="ident", align_bytes=64)
-        first_ident = keep.tile([P, P], F32, name="first_ident", tag="planes", align_bytes=64)
+        planes = keep.tile([P, PASSES * N // WORD], I32, name="planes", align_bytes=64)
 
         def zero(rows):
             cut = rows.shape[1] // 2 + 1
@@ -58,22 +58,22 @@ def tile_attend_sigprior_srt_kernel(tc, qT, k_words, k_scales, ts, pr, offs, out
 
         zero(scale_pool[QUADRANT : 2 * QUADRANT, :])
         zero(scale_pool[2 * QUADRANT : P, :])
-        make_identity(nc, first_ident[:])
+        zero(planes[:])
         make_identity(nc, ident[:])
-        nc.gpsimd.memset(pr_pool[0:ROW, :], 0.0)
+        nc.gpsimd.memset(pr_pool[0:ROW, :P], 0.0)
+        nc.gpsimd.memset(pr_pool[0:ROW, P:], 0.0)
 
-        def load_queries(o, tag):
-            raw = keep.tile([P, PACK, NQ], F32, name="q_raw%d" % o, tag=tag, align_bytes=64)
+        def load_queries(o, raw):
             rows = qT[0, o * P * PACK : (o + 1) * P * PACK, :]
             nc.sync.dma_start(raw[:], rows.rearrange("(p t) q -> p t q", t=PACK))
             return raw
 
         ts_runs = keep.tile([P, RUN], F32, name="ts_runs", align_bytes=64)
-        nc.sync.dma_start(ts_runs[:], ts[0].rearrange("(p j) -> p j", j=RUN))
         nc.sync.dma_start(offsets[:], offs)
         nc.sync.dma_start(scale_pool[0:QUADRANT, :], k_scales.bitcast(I32).rearrange("o f t -> f o t"))
+        nc.sync.dma_start(ts_runs[:], ts[0].rearrange("(p j) -> p j", j=RUN))
         nc.sync.dma_start(pr_pool[ROW:P, :], pr[0:1, :])
-        q_raw = [load_queries(0, "q_raw0")]
+        q_raw = [load_queries(0, shared.tile([P, PACK, NQ], F32, name="q_raw0", align_bytes=64, offset=0))]
         all_words = k_words[0].rearrange("p t b -> p (t b)").bitcast(I32)
         nc.sync.dma_start(word_pool[:, :PREFIX], all_words[:, :PREFIX])
         nc.sync.dma_start(word_pool[:, PREFIX:], all_words[:, PREFIX:])
@@ -83,17 +83,15 @@ def tile_attend_sigprior_srt_kernel(tc, qT, k_words, k_scales, ts, pr, offs, out
             bank = psum.tile([P, BANK, P], F32, name="ts_bank%d" % b, tag="ts_bank%d" % b)
             for j in range(BANK):
                 column = ts_runs[:, b * BANK + j : b * BANK + j + 1]
-                nc.tensor.transpose(bank[:, j, :], column.to_broadcast([P, P]), (first_ident if b < 2 else ident)[:])
+                nc.tensor.transpose(bank[:, j, :], column.to_broadcast([P, P]), ident[:])
             nc.scalar.copy(ts_tokens[:, :, b * BANK : (b + 1) * BANK], bank[:].rearrange("m j p -> m p j"))
 
-        planes = keep.tile([P, PASSES * N // WORD], I32, name="planes", tag="planes", align_bytes=64)
-        nc.gpsimd.memset(planes[:], 0)
         picked_scales = keep.tile([P, N], U8, name="picked_scales", align_bytes=64)
         nc.vector.tensor_copy(picked_scales[:], scale_pool[:].bitcast(U8).indirect(offsets[:]))
         for g in range(P // QUADRANT):
             scale_rows = picked_scales[g * PASSES * SCALE_ROWS : (g + 1) * PASSES * SCALE_ROWS, :]
-            nc.scalar.dma_start(planes[g * QUADRANT : g * QUADRANT + SCALE_ROWS, :], scale_rows.bitcast(I32))
-        q_raw.append(load_queries(1, "q_raw1"))
+            nc.sync.dma_start(planes[g * QUADRANT : g * QUADRANT + SCALE_ROWS, :], scale_rows.bitcast(I32))
+        q_raw.append(load_queries(1, keep.tile([P, PACK, NQ], F32, name="q_raw1", tag="scale_pool", align_bytes=64)))
 
         picked_pr = shared.tile([P, N], F32, name="picked_pr", align_bytes=64, offset=WORD * T)
         nc.vector.tensor_copy(picked_pr[:], pr_pool[:].indirect(offsets[:]))
@@ -105,18 +103,6 @@ def tile_attend_sigprior_srt_kernel(tc, qT, k_words, k_scales, ts, pr, offs, out
         half_pr = psum.tile([P, N], F32, name="half_pr", tag="ts_bank1")
         for j in range(BLOCKS):
             nc.tensor.transpose(half_pr[:, j * P : (j + 1) * P], cols[:, j : j + 1].to_broadcast([P, P]), ident[:])
-
-        k_codes = keep.tile([P, PASSES, N], U16, name="k_codes", align_bytes=64)
-        words = []
-        for a in range(PARTS):
-            gathered = shared.tile([P, PART], U32, name="words%d" % a, align_bytes=64, offset=WORD * PART * a)
-            entries = offsets[:, a * PART // GROUP : (a + 1) * PART // GROUP]
-            window = word_pool[:, : T - N + (a + 1) * PART]
-            nc.vector.tensor_copy(gathered[:], window.bitcast(U32).indirect(entries))
-            words.append(gathered)
-        for a in range(PARTS):
-            pairs = words[a][:].bitcast(U16).rearrange("p (n o) -> p o n", o=PASSES)
-            nc.vector.tensor_copy(k_codes[:, :, a * PART : (a + 1) * PART], pairs)
 
         grouped = {}
         for o in range(PASSES):
@@ -139,26 +125,32 @@ def tile_attend_sigprior_srt_kernel(tc, qT, k_words, k_scales, ts, pr, offs, out
         def round_on_gpsimd(to, rows):
             nc.gpsimd.tensor_scalar(to, rows, 1.0, 0.0, op0=MULT, op1=ADD)
 
-        def score(o, h):
+        def quantise(o, h):
             name = "q_codes%d%d" % (o, h)
             codes = keep.tile([P, P], U32, name=name, align_bytes=64)
             scales = keep.tile([P, P], U8, name="q_scales%d%d" % (o, h), align_bytes=64)
             flat = grouped[o, h].rearrange("p q t -> p (q t)")
             nc.vector.quantize_mx(out=codes[:].bitcast(FP8X4), scales=scales[:], in_=flat)
+            return codes, scales
+
+        def multiply(o, h, codes, scales):
             for a in range(PARTS):
                 first = (o * N + a * PART) // WORD
                 nc.tensor.matmul_mx(
                     out=scores[h, a][:],
                     lhsT=codes[:].bitcast(FP8X4),
                     lhsT_scale=scales[:],
-                    rhs=k_codes[:, o, a * PART : (a + 1) * PART].bitcast(FP4X4),
+                    rhs=keys[a][:, o, :].bitcast(FP4X4),
                     rhs_scale=planes[:, first : first + PART // WORD].bitcast(U8),
                     start=(o == 0),
                     stop=(o == PASSES - 1),
                 )
 
         def pick_ts(a):
-            part = keep.tile([P, PART], F32, name="ts_part%d" % a, align_bytes=64)
+            if a == 0:
+                part = keep.tile([P, PART], F32, name="ts_part0", align_bytes=64)
+            else:
+                part = shared.tile([P, PART], F32, name="ts_part1", align_bytes=64, offset=0)
             entries = offsets[:, a * PART // GROUP : (a + 1) * PART // GROUP]
             if a == 0:
                 nc.scalar.activation(part[:], ts_pool[:].indirect(entries), COPY)
@@ -167,17 +159,30 @@ def tile_attend_sigprior_srt_kernel(tc, qT, k_words, k_scales, ts, pr, offs, out
             return part
 
         ts_parts = [pick_ts(0)]
-        for o in range(PASSES):
-            for h in range(HALVES):
-                if o == 0:
-                    round_on_gpsimd(grouped[o, h], q_raw[o][:, :, h * P : (h + 1) * P].rearrange("p t q -> p q t"))
-                else:
-                    interleave(o, h, nc.scalar.copy)
-        score(0, 0)
-        score(0, 1)
+        first_pass = []
+        for h in range(HALVES):
+            round_on_gpsimd(grouped[0, h], q_raw[0][:, :, h * P : (h + 1) * P].rearrange("p t q -> p q t"))
+            first_pass.append(quantise(0, h))
+
+        words = []
+        for a in range(PARTS):
+            gathered = shared.tile([P, PART], U32, name="words%d" % a, align_bytes=64, offset=WORD * PART * a)
+            entries = offsets[:, a * PART // GROUP : (a + 1) * PART // GROUP]
+            window = word_pool[:, : T - N + (a + 1) * PART]
+            nc.vector.tensor_copy(gathered[:], window.bitcast(U32).indirect(entries))
+            words.append(gathered)
+        keys = []
+        for a in range(PARTS):
+            k_codes = keep.tile([P, PASSES, PART], U16, name="k_codes%d" % a, align_bytes=64)
+            nc.vector.tensor_copy(k_codes[:], words[a][:].bitcast(U16).rearrange("p (n o) -> p o n", o=PASSES))
+            keys.append(k_codes)
+
+        for h in range(HALVES):
+            multiply(0, h, *first_pass[h])
         ts_parts.append(pick_ts(1))
-        score(1, 0)
-        score(1, 1)
+        for h in range(HALVES):
+            interleave(1, h, nc.scalar.copy)
+            multiply(1, h, *quantise(1, h))
 
         pieces = [(h, a) for h in range(HALVES) for a in range(PARTS)]
         gates = []

@@ -34,6 +34,8 @@ PART = N // PARTS
 RUN = T // P
 PREFIX = T - N + PART
 BANK = 4
+GROUPED = 2 * P * PACK
+LATE = WORD * T + WORD * N + GROUPED
 
 
 def tile_attend_sigprior_srt_kernel(tc, qT, k_words, k_scales, ts, pr, offs, out):
@@ -49,7 +51,7 @@ def tile_attend_sigprior_srt_kernel(tc, qT, k_words, k_scales, ts, pr, offs, out
         pr_pool = keep.tile([P, T], F32, name="pr_pool", align_bytes=64)
         word_pool = keep.tile([P, T], I32, name="word_pool", align_bytes=64)
         ident = keep.tile([P, P], F32, name="ident", align_bytes=64)
-        planes = keep.tile([P, PASSES * N // WORD], I32, name="planes", align_bytes=64)
+        first_ident = keep.tile([P, P], F32, name="first_ident", tag="planes", align_bytes=64)
 
         def zero(rows):
             cut = rows.shape[1] // 2 + 1
@@ -58,10 +60,10 @@ def tile_attend_sigprior_srt_kernel(tc, qT, k_words, k_scales, ts, pr, offs, out
 
         zero(scale_pool[QUADRANT : 2 * QUADRANT, :])
         zero(scale_pool[2 * QUADRANT : P, :])
-        zero(planes[:])
+        make_identity(nc, first_ident[:])
         make_identity(nc, ident[:])
-        nc.gpsimd.memset(pr_pool[0:ROW, :P], 0.0)
-        nc.gpsimd.memset(pr_pool[0:ROW, P:], 0.0)
+        zero(pr_pool[0:ROW, :N])
+        nc.gpsimd.memset(pr_pool[0:ROW, N:], 0.0)
 
         def load_queries(o, raw):
             rows = qT[0, o * P * PACK : (o + 1) * P * PACK, :]
@@ -69,9 +71,9 @@ def tile_attend_sigprior_srt_kernel(tc, qT, k_words, k_scales, ts, pr, offs, out
             return raw
 
         ts_runs = keep.tile([P, RUN], F32, name="ts_runs", align_bytes=64)
+        nc.sync.dma_start(ts_runs[:], ts[0].rearrange("(p j) -> p j", j=RUN))
         nc.sync.dma_start(offsets[:], offs)
         nc.sync.dma_start(scale_pool[0:QUADRANT, :], k_scales.bitcast(I32).rearrange("o f t -> f o t"))
-        nc.sync.dma_start(ts_runs[:], ts[0].rearrange("(p j) -> p j", j=RUN))
         nc.sync.dma_start(pr_pool[ROW:P, :], pr[0:1, :])
         q_raw = [load_queries(0, shared.tile([P, PACK, NQ], F32, name="q_raw0", align_bytes=64, offset=0))]
         all_words = k_words[0].rearrange("p t b -> p (t b)").bitcast(I32)
@@ -83,23 +85,25 @@ def tile_attend_sigprior_srt_kernel(tc, qT, k_words, k_scales, ts, pr, offs, out
             bank = psum.tile([P, BANK, P], F32, name="ts_bank%d" % b, tag="ts_bank%d" % b)
             for j in range(BANK):
                 column = ts_runs[:, b * BANK + j : b * BANK + j + 1]
-                nc.tensor.transpose(bank[:, j, :], column.to_broadcast([P, P]), ident[:])
+                nc.tensor.transpose(bank[:, j, :], column.to_broadcast([P, P]), (first_ident if b == 0 else ident)[:])
             nc.scalar.copy(ts_tokens[:, :, b * BANK : (b + 1) * BANK], bank[:].rearrange("m j p -> m p j"))
 
+        planes = keep.tile([P, PASSES * N // WORD], I32, name="planes", tag="planes", align_bytes=64)
+        nc.gpsimd.memset(planes[:], 0)
         picked_scales = keep.tile([P, N], U8, name="picked_scales", align_bytes=64)
         nc.vector.tensor_copy(picked_scales[:], scale_pool[:].bitcast(U8).indirect(offsets[:]))
         for g in range(P // QUADRANT):
             scale_rows = picked_scales[g * PASSES * SCALE_ROWS : (g + 1) * PASSES * SCALE_ROWS, :]
-            nc.sync.dma_start(planes[g * QUADRANT : g * QUADRANT + SCALE_ROWS, :], scale_rows.bitcast(I32))
-        q_raw.append(load_queries(1, keep.tile([P, PACK, NQ], F32, name="q_raw1", tag="scale_pool", align_bytes=64)))
+            nc.scalar.dma_start(planes[g * QUADRANT : g * QUADRANT + SCALE_ROWS, :], scale_rows.bitcast(I32))
+        q_raw.append(load_queries(1, keep.tile([P, PACK, NQ], F32, name="q_raw1", tag="q_raw1", align_bytes=64)))
 
         picked_pr = shared.tile([P, N], F32, name="picked_pr", align_bytes=64, offset=WORD * T)
         nc.vector.tensor_copy(picked_pr[:], pr_pool[:].indirect(offsets[:]))
         turned = psum.tile([P, BLOCKS, P], F32, name="turned", tag="ts_bank0")
         for j in range(BLOCKS):
             nc.tensor.transpose(turned[:, j, :], picked_pr[:, j * P : (j + 1) * P], ident[:])
-        cols = keep.tile([P, BLOCKS], F32, name="cols", align_bytes=64)
-        nc.scalar.activation(cols[:], turned[:, :, ROW], COPY, scale=0.5)
+        cols = shared.tile([P, GROUP], F32, name="cols", offset=LATE + GROUPED - 32)[:, :BLOCKS]
+        nc.scalar.activation(cols, turned[:, :, ROW], COPY, scale=0.5)
         half_pr = psum.tile([P, N], F32, name="half_pr", tag="ts_bank1")
         for j in range(BLOCKS):
             nc.tensor.transpose(half_pr[:, j * P : (j + 1) * P], cols[:, j : j + 1].to_broadcast([P, P]), ident[:])
@@ -109,7 +113,7 @@ def tile_attend_sigprior_srt_kernel(tc, qT, k_words, k_scales, ts, pr, offs, out
             for h in range(HALVES):
                 name = "grouped%d%d" % (o, h)
                 if o == 1:
-                    place = WORD * T + 2 * P * PACK * h
+                    place = LATE + GROUPED * h
                     grouped[o, h] = shared.tile([P, P, PACK], BF16, name=name, align_bytes=64, offset=place)[:]
                 else:
                     grouped[o, h] = keep.tile([P, P, PACK], BF16, name=name, align_bytes=64)[:]
@@ -133,22 +137,22 @@ def tile_attend_sigprior_srt_kernel(tc, qT, k_words, k_scales, ts, pr, offs, out
             nc.vector.quantize_mx(out=codes[:].bitcast(FP8X4), scales=scales[:], in_=flat)
             return codes, scales
 
-        def multiply(o, h, codes, scales):
-            for a in range(PARTS):
-                first = (o * N + a * PART) // WORD
-                nc.tensor.matmul_mx(
-                    out=scores[h, a][:],
-                    lhsT=codes[:].bitcast(FP8X4),
-                    lhsT_scale=scales[:],
-                    rhs=keys[a][:, o, :].bitcast(FP4X4),
-                    rhs_scale=planes[:, first : first + PART // WORD].bitcast(U8),
-                    start=(o == 0),
-                    stop=(o == PASSES - 1),
-                )
+        def multiply(o, h, a):
+            codes, scales = queries[o, h]
+            first = (o * N + a * PART) // WORD
+            nc.tensor.matmul_mx(
+                out=scores[h, a][:],
+                lhsT=codes[:].bitcast(FP8X4),
+                lhsT_scale=scales[:],
+                rhs=keys[a][:, o, :].bitcast(FP4X4),
+                rhs_scale=planes[:, first : first + PART // WORD].bitcast(U8),
+                start=(o == 0),
+                stop=(o == PASSES - 1),
+            )
 
         def pick_ts(a):
             if a == 0:
-                part = keep.tile([P, PART], F32, name="ts_part0", align_bytes=64)
+                part = shared.tile([P, PART], F32, name="ts_part0", align_bytes=64, offset=WORD * T)
             else:
                 part = shared.tile([P, PART], F32, name="ts_part1", align_bytes=64, offset=0)
             entries = offsets[:, a * PART // GROUP : (a + 1) * PART // GROUP]
@@ -159,10 +163,10 @@ def tile_attend_sigprior_srt_kernel(tc, qT, k_words, k_scales, ts, pr, offs, out
             return part
 
         ts_parts = [pick_ts(0)]
-        first_pass = []
+        queries = {}
         for h in range(HALVES):
             round_on_gpsimd(grouped[0, h], q_raw[0][:, :, h * P : (h + 1) * P].rearrange("p t q -> p q t"))
-            first_pass.append(quantise(0, h))
+            queries[0, h] = quantise(0, h)
 
         words = []
         for a in range(PARTS):
@@ -177,12 +181,14 @@ def tile_attend_sigprior_srt_kernel(tc, qT, k_words, k_scales, ts, pr, offs, out
             nc.vector.tensor_copy(k_codes[:], words[a][:].bitcast(U16).rearrange("p (n o) -> p o n", o=PASSES))
             keys.append(k_codes)
 
-        for h in range(HALVES):
-            multiply(0, h, *first_pass[h])
         ts_parts.append(pick_ts(1))
         for h in range(HALVES):
             interleave(1, h, nc.scalar.copy)
-            multiply(1, h, *quantise(1, h))
+            queries[1, h] = quantise(1, h)
+        for h in range(HALVES):
+            for o in range(PASSES):
+                for a in range(PARTS):
+                    multiply(o, h, a)
 
         pieces = [(h, a) for h in range(HALVES) for a in range(PARTS)]
         gates = []

@@ -35,7 +35,8 @@ RUN = T // P
 PREFIX = T - N + PART
 BANK = 4
 GROUPED = 2 * P * PACK
-LATE = WORD * T + WORD * N + GROUPED
+PR_POOL = WORD * PACK * NQ
+LATE = PR_POOL + WORD * T + WORD * PART
 
 
 def tile_attend_sigprior_srt_kernel(tc, qT, k_words, k_scales, ts, pr, offs, out):
@@ -48,7 +49,7 @@ def tile_attend_sigprior_srt_kernel(tc, qT, k_words, k_scales, ts, pr, offs, out
         offsets = keep.tile([P, N // GROUP], U16, name="offsets")
         scale_pool = keep.tile([P, T // WORD], I32, name="scale_pool", tag="scale_pool", align_bytes=64)
         ts_pool = keep.tile([P, T], F32, name="ts_pool", align_bytes=64)
-        pr_pool = keep.tile([P, T], F32, name="pr_pool", align_bytes=64)
+        pr_pool = shared.tile([P, T], F32, name="pr_pool", align_bytes=64, offset=PR_POOL)
         word_pool = keep.tile([P, T], I32, name="word_pool", align_bytes=64)
         ident = keep.tile([P, P], F32, name="ident", align_bytes=64)
         first_ident = keep.tile([P, P], F32, name="first_ident", tag="planes", align_bytes=64)
@@ -97,13 +98,13 @@ def tile_attend_sigprior_srt_kernel(tc, qT, k_words, k_scales, ts, pr, offs, out
             nc.scalar.dma_start(planes[g * QUADRANT : g * QUADRANT + SCALE_ROWS, :], scale_rows.bitcast(I32))
         q_raw.append(load_queries(1, keep.tile([P, PACK, NQ], F32, name="q_raw1", tag="q_raw1", align_bytes=64)))
 
-        picked_pr = shared.tile([P, N], F32, name="picked_pr", align_bytes=64, offset=WORD * T)
+        picked_pr = shared.tile([P, N], F32, name="picked_pr", align_bytes=64, offset=LATE - 64)
         nc.vector.tensor_copy(picked_pr[:], pr_pool[:].indirect(offsets[:]))
         turned = psum.tile([P, BLOCKS, P], F32, name="turned", tag="ts_bank0")
         for j in range(BLOCKS):
             nc.tensor.transpose(turned[:, j, :], picked_pr[:, j * P : (j + 1) * P], ident[:])
-        cols = shared.tile([P, GROUP], F32, name="cols", offset=LATE + GROUPED - 32)[:, :BLOCKS]
-        nc.scalar.activation(cols, turned[:, :, ROW], COPY, scale=0.5)
+        cols = keep.tile([P, BLOCKS], F32, name="cols", align_bytes=64)
+        nc.scalar.activation(cols[:], turned[:, :, ROW], COPY, scale=0.5)
         half_pr = psum.tile([P, N], F32, name="half_pr", tag="ts_bank1")
         for j in range(BLOCKS):
             nc.tensor.transpose(half_pr[:, j * P : (j + 1) * P], cols[:, j : j + 1].to_broadcast([P, P]), ident[:])
@@ -112,11 +113,8 @@ def tile_attend_sigprior_srt_kernel(tc, qT, k_words, k_scales, ts, pr, offs, out
         for o in range(PASSES):
             for h in range(HALVES):
                 name = "grouped%d%d" % (o, h)
-                if o == 1:
-                    place = LATE + GROUPED * h
-                    grouped[o, h] = shared.tile([P, P, PACK], BF16, name=name, align_bytes=64, offset=place)[:]
-                else:
-                    grouped[o, h] = keep.tile([P, P, PACK], BF16, name=name, align_bytes=64)[:]
+                place = (LATE if o else PR_POOL) + GROUPED * h
+                grouped[o, h] = shared.tile([P, P, PACK], BF16, name=name, align_bytes=64, offset=place)[:]
         scores = {}
         for h in range(HALVES):
             for a in range(PARTS):
@@ -125,9 +123,6 @@ def tile_attend_sigprior_srt_kernel(tc, qT, k_words, k_scales, ts, pr, offs, out
         def interleave(o, h, copy):
             rows = q_raw[o][:, :, h * P : (h + 1) * P].rearrange("p t (c i) -> p c t i", i=PACK)
             copy(grouped[o, h].rearrange("p (c i) t -> p c t i", i=PACK), rows)
-
-        def round_on_gpsimd(to, rows):
-            nc.gpsimd.tensor_scalar(to, rows, 1.0, 0.0, op0=MULT, op1=ADD)
 
         def quantise(o, h):
             name = "q_codes%d%d" % (o, h)
@@ -152,7 +147,7 @@ def tile_attend_sigprior_srt_kernel(tc, qT, k_words, k_scales, ts, pr, offs, out
 
         def pick_ts(a):
             if a == 0:
-                part = shared.tile([P, PART], F32, name="ts_part0", align_bytes=64, offset=WORD * T)
+                part = shared.tile([P, PART], F32, name="ts_part0", align_bytes=64, offset=LATE - WORD * PART)
             else:
                 part = shared.tile([P, PART], F32, name="ts_part1", align_bytes=64, offset=0)
             entries = offsets[:, a * PART // GROUP : (a + 1) * PART // GROUP]
@@ -165,7 +160,8 @@ def tile_attend_sigprior_srt_kernel(tc, qT, k_words, k_scales, ts, pr, offs, out
         ts_parts = [pick_ts(0)]
         queries = {}
         for h in range(HALVES):
-            round_on_gpsimd(grouped[0, h], q_raw[0][:, :, h * P : (h + 1) * P].rearrange("p t q -> p q t"))
+            interleave(0, h, nc.vector.tensor_copy)
+        for h in range(HALVES):
             queries[0, h] = quantise(0, h)
 
         words = []
@@ -185,8 +181,8 @@ def tile_attend_sigprior_srt_kernel(tc, qT, k_words, k_scales, ts, pr, offs, out
         for h in range(HALVES):
             interleave(1, h, nc.scalar.copy)
             queries[1, h] = quantise(1, h)
-        for h in range(HALVES):
-            for o in range(PASSES):
+        for o in range(PASSES):
+            for h in range(HALVES):
                 for a in range(PARTS):
                     multiply(o, h, a)
 

from contextlib import ExitStack

import concourse.mybir as mybir
from concourse.masks import make_identity

N, T, D, NQ = 512, 2048, 1024, 256
FLOPS = 2 * NQ * N * D

F32 = mybir.dt.float32
BF16 = mybir.dt.bfloat16
I32 = mybir.dt.int32
U32 = mybir.dt.uint32
U16 = mybir.dt.uint16
U8 = mybir.dt.uint8
FP8X4 = mybir.dt.float8_e4m3fn_x4
FP4X4 = mybir.dt.float4_e2m1fn_x4
MULT = mybir.AluOpType.mult
ADD = mybir.AluOpType.add
TANH = mybir.ActivationFunctionType.Tanh
COPY = mybir.ActivationFunctionType.Copy

P = 128
PACK = 4
PASSES = D // (P * PACK)
HALVES = NQ // P
BLOCKS = N // P
GROUP = 16
QUADRANT = 32
SCALE_ROWS = 4
WORD = 4
ROW = P - 1
PARTS = 2
PART = N // PARTS
RUN = T // P
PREFIX = T - N + PART
BANK = 4
GROUPED = 2 * P * PACK
PR_POOL = WORD * PACK * NQ
LATE = PR_POOL + WORD * T + WORD * PART


def tile_attend_sigprior_srt_kernel(tc, qT, k_words, k_scales, ts, pr, offs, out):
    nc = tc.nc
    with ExitStack() as ctx:
        keep = ctx.enter_context(tc.tile_pool(name="keep", bufs=1))
        shared = ctx.enter_context(tc.tile_pool(name="shared", bufs=1))
        psum = ctx.enter_context(tc.psum_pool(name="psum", bufs=1))

        offsets = keep.tile([P, N // GROUP], U16, name="offsets")
        scale_pool = keep.tile([P, T // WORD], I32, name="scale_pool", tag="scale_pool", align_bytes=64)
        ts_pool = keep.tile([P, T], F32, name="ts_pool", align_bytes=64)
        pr_pool = shared.tile([P, T], F32, name="pr_pool", align_bytes=64, offset=PR_POOL)
        word_pool = keep.tile([P, T], I32, name="word_pool", align_bytes=64)
        ident = keep.tile([P, P], F32, name="ident", align_bytes=64)
        first_ident = keep.tile([P, P], F32, name="first_ident", tag="planes", align_bytes=64)

        def zero(rows):
            cut = rows.shape[1] // 2 + 1
            nc.vector.memset(rows[:, :cut], 0)
            nc.vector.memset(rows[:, cut:], 0)

        zero(scale_pool[QUADRANT : 2 * QUADRANT, :])
        zero(scale_pool[2 * QUADRANT : P, :])
        make_identity(nc, first_ident[:])
        make_identity(nc, ident[:])
        zero(pr_pool[0:ROW, :N])
        nc.gpsimd.memset(pr_pool[0:ROW, N:], 0.0)

        def load_queries(o, raw):
            rows = qT[0, o * P * PACK : (o + 1) * P * PACK, :]
            nc.sync.dma_start(raw[:], rows.rearrange("(p t) q -> p t q", t=PACK))
            return raw

        ts_runs = keep.tile([P, RUN], F32, name="ts_runs", align_bytes=64)
        nc.sync.dma_start(ts_runs[:], ts[0].rearrange("(p j) -> p j", j=RUN))
        nc.sync.dma_start(offsets[:], offs)
        nc.sync.dma_start(scale_pool[0:QUADRANT, :], k_scales.bitcast(I32).rearrange("o f t -> f o t"))
        nc.sync.dma_start(pr_pool[ROW:P, :], pr[0:1, :])
        q_raw = [load_queries(0, shared.tile([P, PACK, NQ], F32, name="q_raw0", align_bytes=64, offset=0))]
        all_words = k_words[0].rearrange("p t b -> p (t b)").bitcast(I32)
        nc.sync.dma_start(word_pool[:, :PREFIX], all_words[:, :PREFIX])
        nc.sync.dma_start(word_pool[:, PREFIX:], all_words[:, PREFIX:])

        ts_tokens = ts_pool[:].rearrange("m (p j) -> m p j", j=RUN)
        for b in range(RUN // BANK):
            bank = psum.tile([P, BANK, P], F32, name="ts_bank%d" % b, tag="ts_bank%d" % b)
            for j in range(BANK):
                column = ts_runs[:, b * BANK + j : b * BANK + j + 1]
                nc.tensor.transpose(bank[:, j, :], column.to_broadcast([P, P]), (first_ident if b == 0 else ident)[:])
            nc.scalar.copy(ts_tokens[:, :, b * BANK : (b + 1) * BANK], bank[:].rearrange("m j p -> m p j"))

        planes = keep.tile([P, PASSES * N // WORD], I32, name="planes", tag="planes", align_bytes=64)
        nc.gpsimd.memset(planes[:], 0)
        picked_scales = keep.tile([P, N], U8, name="picked_scales", align_bytes=64)
        nc.vector.tensor_copy(picked_scales[:], scale_pool[:].bitcast(U8).indirect(offsets[:]))
        for g in range(P // QUADRANT):
            scale_rows = picked_scales[g * PASSES * SCALE_ROWS : (g + 1) * PASSES * SCALE_ROWS, :]
            nc.scalar.dma_start(planes[g * QUADRANT : g * QUADRANT + SCALE_ROWS, :], scale_rows.bitcast(I32))
        q_raw.append(load_queries(1, keep.tile([P, PACK, NQ], F32, name="q_raw1", tag="q_raw1", align_bytes=64)))

        picked_pr = shared.tile([P, N], F32, name="picked_pr", align_bytes=64, offset=LATE - 64)
        nc.vector.tensor_copy(picked_pr[:], pr_pool[:].indirect(offsets[:]))
        turned = psum.tile([P, BLOCKS, P], F32, name="turned", tag="ts_bank0")
        for j in range(BLOCKS):
            nc.tensor.transpose(turned[:, j, :], picked_pr[:, j * P : (j + 1) * P], ident[:])
        cols = keep.tile([P, BLOCKS], F32, name="cols", align_bytes=64)
        nc.scalar.activation(cols[:], turned[:, :, ROW], COPY, scale=0.5)
        half_pr = psum.tile([P, N], F32, name="half_pr", tag="ts_bank1")
        for j in range(BLOCKS):
            nc.tensor.transpose(half_pr[:, j * P : (j + 1) * P], cols[:, j : j + 1].to_broadcast([P, P]), ident[:])

        grouped = {}
        for o in range(PASSES):
            for h in range(HALVES):
                name = "grouped%d%d" % (o, h)
                place = (LATE if o else PR_POOL) + GROUPED * h
                grouped[o, h] = shared.tile([P, P, PACK], BF16, name=name, align_bytes=64, offset=place)[:]
        scores = {}
        for h in range(HALVES):
            for a in range(PARTS):
                scores[h, a] = psum.tile([P, PART], F32, name="scores%d%d" % (h, a))

        def interleave(o, h, copy):
            rows = q_raw[o][:, :, h * P : (h + 1) * P].rearrange("p t (c i) -> p c t i", i=PACK)
            copy(grouped[o, h].rearrange("p (c i) t -> p c t i", i=PACK), rows)

        def quantise(o, h):
            name = "q_codes%d%d" % (o, h)
            codes = keep.tile([P, P], U32, name=name, align_bytes=64)
            scales = keep.tile([P, P], U8, name="q_scales%d%d" % (o, h), align_bytes=64)
            flat = grouped[o, h].rearrange("p q t -> p (q t)")
            nc.vector.quantize_mx(out=codes[:].bitcast(FP8X4), scales=scales[:], in_=flat)
            return codes, scales

        def multiply(o, h, a):
            codes, scales = queries[o, h]
            first = (o * N + a * PART) // WORD
            nc.tensor.matmul_mx(
                out=scores[h, a][:],
                lhsT=codes[:].bitcast(FP8X4),
                lhsT_scale=scales[:],
                rhs=keys[a][:, o, :].bitcast(FP4X4),
                rhs_scale=planes[:, first : first + PART // WORD].bitcast(U8),
                start=(o == 0),
                stop=(o == PASSES - 1),
            )

        def pick_ts(a):
            if a == 0:
                part = shared.tile([P, PART], F32, name="ts_part0", align_bytes=64, offset=LATE - WORD * PART)
            else:
                part = shared.tile([P, PART], F32, name="ts_part1", align_bytes=64, offset=0)
            entries = offsets[:, a * PART // GROUP : (a + 1) * PART // GROUP]
            if a == 0:
                nc.scalar.activation(part[:], ts_pool[:].indirect(entries), COPY)
            else:
                nc.vector.tensor_copy(part[:], ts_pool[:].indirect(entries))
            return part

        ts_parts = [pick_ts(0)]
        queries = {}
        for h in range(HALVES):
            interleave(0, h, nc.vector.tensor_copy)
        for h in range(HALVES):
            queries[0, h] = quantise(0, h)

        words = []
        for a in range(PARTS):
            gathered = shared.tile([P, PART], U32, name="words%d" % a, align_bytes=64, offset=WORD * PART * a)
            entries = offsets[:, a * PART // GROUP : (a + 1) * PART // GROUP]
            window = word_pool[:, : T - N + (a + 1) * PART]
            nc.vector.tensor_copy(gathered[:], window.bitcast(U32).indirect(entries))
            words.append(gathered)
        keys = []
        for a in range(PARTS):
            k_codes = keep.tile([P, PASSES, PART], U16, name="k_codes%d" % a, align_bytes=64)
            nc.vector.tensor_copy(k_codes[:], words[a][:].bitcast(U16).rearrange("p (n o) -> p o n", o=PASSES))
            keys.append(k_codes)

        ts_parts.append(pick_ts(1))
        for h in range(HALVES):
            interleave(1, h, nc.scalar.copy)
            queries[1, h] = quantise(1, h)
        for o in range(PASSES):
            for h in range(HALVES):
                for a in range(PARTS):
                    multiply(o, h, a)

        pieces = [(h, a) for h in range(HALVES) for a in range(PARTS)]
        gates = []
        for i, (h, a) in enumerate(pieces):
            scaled = keep.tile([P, PART], F32, name="scaled%d" % i, align_bytes=64)
            nc.vector.tensor_tensor(scaled[:], scores[h, a][:], ts_parts[a][:], MULT)
            gate = keep.tile([P, PART], F32, name="gate%d" % i, align_bytes=64)
            nc.scalar.activation(gate[:], scaled[:], TANH, scale=0.5)
            gates.append(gate)
        for i, (h, a) in enumerate(pieces):
            slots = slice(a * PART, (a + 1) * PART)
            result = keep.tile([P, PART], F32, name="result%d" % i, align_bytes=64)
            nc.vector.scalar_tensor_tensor(result[:], gates[i][:], 1.0, half_pr[:, slots], op0=ADD, op1=MULT)
            nc.sync.dma_start(out[0, h * P : (h + 1) * P, slots], result[:])
